import numpy as np
import ml_dtypes


def mxq(x, axis, fmt="e4m3"):
    dtype, down = {"e4m3": (ml_dtypes.float8_e4m3fn, 7), "e5m2": (ml_dtypes.float8_e5m2, 14)}[fmt]
    v = np.moveaxis(np.asarray(x, np.float32).astype(ml_dtypes.bfloat16).astype(np.float64), axis, -1)
    blocks = v.reshape(v.shape[:-1] + (-1, 32))
    amax = np.abs(blocks).max(-1, keepdims=True)
    byte = np.maximum(np.where(amax > 0, np.frexp(amax)[1] - 1 + 127, 0) - down, 1)
    scale = np.exp2(byte - 127.0)
    codes = (blocks / scale).astype(np.float32).astype(dtype).astype(np.float64)
    return np.moveaxis((codes * scale).reshape(v.shape), -1, axis)


WIDE = False


def mx_kscale(k):
    if not WIDE:
        return np.ones(k)
    levels = np.array([10, -10, 5, -5, 0])
    if k % 512:
        return np.exp2(np.random.permutation(np.resize(levels, k // 32))).repeat(32)
    a = np.empty((k // 512, 16))
    for p in range(k // 512):
        a[p, :8] = np.random.permutation(np.resize(levels, 8))
        for g in range(8):
            far = levels[np.abs(levels - a[p, g]) >= 10]
            a[p, g + 8] = far[np.random.randint(len(far))]
    return np.exp2(a.ravel()).repeat(32)


def f64(x):
    return np.asarray(x).astype(np.float64)


def split(x):
    m, e = np.frexp(f64(x))
    hi = np.ldexp(np.trunc(16.0 * m) / 16.0, e)
    return hi, f64(x) - hi


def silu(v):
    return v / (1.0 + np.exp(-np.maximum(v, -700.0)))


K, M, T = 1536, 512, 512


def setup_inputs():
    n = np.random.standard_normal
    s = mx_kscale(K)[:, None]
    return {
        "w": (n((K, M)) / np.sqrt(K) / s).astype(np.float32),
        "x": (n((K, T)) * s).astype(np.float32),
        "b": (0.3 * n(512)).astype(np.float32),
    }


def reference(w, x, b):
    w_hi, w_lo = split(w)
    w_hi_, w_lo_ = mxq(w_hi, 0, "e4m3"), mxq(w_lo, 0, "e4m3")
    x_ = mxq(f64(x), 0, "e4m3")
    y = w_hi_.T @ x_ + w_lo_.T @ x_
    return silu(y + f64(b)[:, None])

@@ -1,0 +1,243 @@
+from contextlib import ExitStack
+
+import concourse.mybir as mybir
+from concourse.masks import make_identity
+
+K, M, T = 1536, 512, 512
+FLOPS = 2 * 2 * K * M * T
+
+F32 = mybir.dt.float32
+BF16 = mybir.dt.bfloat16
+I32 = mybir.dt.int32
+U32 = mybir.dt.uint32
+U8 = mybir.dt.uint8
+FP8X4 = mybir.dt.float8_e4m3fn_x4
+ALU = mybir.AluOpType
+ACT = mybir.ActivationFunctionType
+
+P = 128
+PACK = 4
+K_PASS = P * PACK
+PASSES = K // K_PASS
+TILES = M // P
+
+HI_WORD = -1048576
+HI_PAIR = -983056
+HI_LOW_HALF = 0xFFF0
+
+
+def tile_mix_hilo_fm_silu_kernel(tc, w, x, b, out):
+    nc = tc.nc
+    with ExitStack() as ctx:
+        keep = ctx.enter_context(tc.tile_pool(name="keep", bufs=1))
+        psum = ctx.enter_context(tc.psum_pool(name="psum", bufs=1))
+
+        def keep_tile(name, shape, dtype):
+            t = keep.tile(shape, dtype, name=name, align_bytes=64)
+            return t
+
+        def per_pass(name, shape, dtype):
+            return [keep_tile(name + str(g), shape, dtype) for g in range(PASSES)]
+
+        w_raw = per_pass("w_raw", [P, PACK, M], F32)
+        x_raw = per_pass("x_raw", [P, PACK, T], F32)
+        w_top = per_pass("w_top", [P, M, PACK], BF16)
+        w_even = per_pass("w_even", [P, 2, M], I32)
+        w_hi = per_pass("w_hi", [P, M, 2], I32)
+        w_lo = per_pass("w_lo", [P, M, PACK], BF16)
+        x_bf = per_pass("x_bf", [P, T, PACK], BF16)
+        hi_codes = per_pass("hi_codes", [P, M], U32)
+        hi_scales = per_pass("hi_scales", [P, M], U8)
+        lo_codes = per_pass("lo_codes", [P, M], U32)
+        lo_scales = per_pass("lo_scales", [P, M], U8)
+        x_codes = per_pass("x_codes", [P, T], U32)
+        x_scales = per_pass("x_scales", [P, T], U8)
+        acc = [psum.tile([P, T], F32, name="acc" + str(m)) for m in range(TILES)]
+        res = [keep_tile("res" + str(m), [P, T], F32) for m in range(TILES)]
+
+        warm = keep_tile("warm", [P, 8], F32)
+        b_rows = keep_tile("b_rows", [P, P], F32)
+        b_cols = keep_tile("b_cols", [P, TILES], F32)
+        ident = keep_tile("ident", [P, P], F32)
+        b_turn = psum.tile([P, P], F32, name="b_turn")
+
+        def load(src, dst, g, c0, c1):
+            rows = src[g * K_PASS : (g + 1) * K_PASS, c0:c1]
+            nc.sync.dma_start(out=dst[g][:, :, c0:c1], in_=rows.rearrange("(p j) c -> p j c", j=PACK))
+
+        def grouped(t, g, c0, c1):
+            return t[g][:, c0:c1, :].rearrange("p (c i) t -> p c t i", i=4)
+
+        def by_row(t, g, c0, c1):
+            return t[g][:, :, c0:c1].rearrange("p t (c i) -> p c t i", i=4)
+
+        def top_halves(g, c0, c1):
+            halves = w_raw[g][:].bitcast(BF16)
+            nc.scalar.copy(
+                out=grouped(w_top, g, c0, c1),
+                in_=halves[:, :, 2 * c0 + 1 : 2 * c1 : 2].rearrange("p t (c i) -> p c t i", i=4),
+            )
+
+        def mask_top(g, c0, c1):
+            nc.vector.tensor_scalar(
+                out=w_hi[g][:, c0:c1, :].rearrange("p c u -> p (c u)"),
+                in0=w_top[g][:, c0:c1, :].rearrange("p c t -> p (c t)").bitcast(I32),
+                scalar1=HI_PAIR,
+                scalar2=None,
+                op0=ALU.bitwise_and,
+            )
+
+        def even_rows(g, c0, c1):
+            words = w_raw[g][:].bitcast(I32)
+            nc.vector.tensor_scalar(
+                out=w_even[g][:, :, c0:c1],
+                in0=words[:, 0:4:2, c0:c1],
+                scalar1=16,
+                scalar2=HI_LOW_HALF,
+                op0=ALU.logical_shift_right,
+                op1=ALU.bitwise_and,
+            )
+
+        def odd_rows(g, c0, c1):
+            words = w_raw[g][:].bitcast(I32)
+            nc.vector.scalar_tensor_tensor(
+                out=w_hi[g][:, c0:c1, :],
+                in0=words[:, 1:4:2, c0:c1].rearrange("p u c -> p c u"),
+                scalar=HI_WORD,
+                in1=w_even[g][:, :, c0:c1].rearrange("p u c -> p c u"),
+                op0=ALU.bitwise_and,
+                op1=ALU.bitwise_or,
+            )
+
+        def subtract(g, c0, c1):
+            hi = w_hi[g][:].rearrange("p c u -> p (c u)").bitcast(BF16)[:, PACK * c0 : PACK * c1]
+            nc.vector.tensor_tensor(
+                out=grouped(w_lo, g, c0, c1),
+                in0=by_row(w_raw, g, c0, c1),
+                in1=hi.rearrange("p (c i t) -> p c t i", i=4, t=PACK),
+                op=ALU.subtract,
+            )
+
+        def quantize(codes, scales, src, g, c0, c1):
+            nc.vector.quantize_mx(
+                out=codes[g][:, c0:c1].bitcast(FP8X4),
+                scales=scales[g][:, c0:c1],
+                in_=src,
+            )
+
+        def quantize_hi(g, c0, c1):
+            src = w_hi[g][:].rearrange("p c u -> p (c u)").bitcast(BF16)[:, PACK * c0 : PACK * c1]
+            quantize(hi_codes, hi_scales, src, g, c0, c1)
+
+        def quantize_lo(g, c0, c1):
+            quantize(lo_codes, lo_scales, w_lo[g][:].rearrange("p c t -> p (c t)")[:, PACK * c0 : PACK * c1], g, c0, c1)
+
+        def quantize_x(g, c0, c1):
+            quantize(x_codes, x_scales, x_bf[g][:].rearrange("p c t -> p (c t)")[:, PACK * c0 : PACK * c1], g, c0, c1)
+
+        def round_x(engine_copy, g, c0, c1):
+            engine_copy(out=grouped(x_bf, g, c0, c1), in_=by_row(x_raw, g, c0, c1))
+
+        def multiply(codes, scales, g, m, start=False, stop=False):
+            cols = slice(m * P, (m + 1) * P)
+            nc.tensor.matmul_mx(
+                out=acc[m][:],
+                lhsT=codes[g][:, cols].bitcast(FP8X4),
+                lhsT_scale=scales[g][:, cols],
+                rhs=x_codes[g][:].bitcast(FP8X4),
+                rhs_scale=x_scales[g][:],
+                start=start,
+                stop=stop,
+            )
+
+        def hi_pass(g, m):
+            multiply(hi_codes, hi_scales, g, m, start=(g == 0))
+
+        def lo_pass(g, m):
+            multiply(lo_codes, lo_scales, g, m, stop=(g == PASSES - 1))
+
+        def finish(m, parts=1):
+            for c in range(parts):
+                cols = slice(c * T // parts, (c + 1) * T // parts)
+                nc.scalar.activation(out=res[m][:, cols], in_=acc[m][:, cols], func=ACT.Silu, bias=b_cols[:, m : m + 1], scale=1.0)
+                nc.sync.dma_start(out=out[m * P : (m + 1) * P, cols], in_=res[m][:, cols])
+
+        with tc.manual_schedule():
+            load(w, w_raw, 0, 0, 256)
+            load(w, w_raw, 0, 256, 512)
+            load(w, w_raw, 1, 0, 512)
+            load(x, x_raw, 0, 0, 512)
+            load(x, x_raw, 1, 0, 512)
+            load(w, w_raw, 2, 0, 256)
+            load(x, x_raw, 2, 0, 256)
+            load(x, x_raw, 2, 256, 512)
+            load(w, w_raw, 2, 256, 512)
+            nc.vector.memset(b_rows[:], 0.0)
+            nc.vector.memset(warm[:], 0.0)
+            nc.scalar.dma_start(out=b_rows[0:TILES, :], in_=b.rearrange("(m p) -> m p", p=P))
+            nc.scalar.activation(out=warm[:, 4:8], in_=warm[:, 0:4], func=ACT.Silu)
+            make_identity(nc, ident[:])
+            nc.tensor.transpose(b_turn[:], b_rows[:], ident[:])
+
+            even_rows(0, 0, 256)
+            top_halves(0, 256, 512)
+            odd_rows(0, 0, 256)
+            subtract(0, 0, 256)
+            quantize_hi(0, 0, 256)
+            mask_top(0, 256, 512)
+            quantize_lo(0, 0, 256)
+            subtract(0, 256, 512)
+            quantize_hi(0, 256, 512)
+
+            top_halves(1, 0, 256)
+            top_halves(1, 256, 512)
+            mask_top(1, 0, 256)
+            quantize_lo(0, 256, 512)
+            quantize_hi(1, 0, 256)
+            subtract(1, 0, 256)
+            mask_top(1, 256, 512)
+            quantize_lo(1, 0, 256)
+            subtract(1, 256, 512)
+            round_x(nc.scalar.copy, 0, 0, 512)
+            nc.scalar.copy(out=b_cols[:], in_=b_turn[:, 0:TILES])
+            quantize_x(0, 0, 512)
+            for m in range(TILES):
+                hi_pass(0, m)
+                lo_pass(0, m)
+
+            round_x(nc.scalar.copy, 1, 0, 256)
+            round_x(nc.scalar.copy, 1, 256, 512)
+            round_x(nc.scalar.copy, 2, 0, 256)
+            round_x(nc.scalar.copy, 2, 256, 512)
+            top_halves(2, 256, 384)
+            top_halves(2, 384, 512)
+            quantize_lo(1, 256, 512)
+            even_rows(2, 0, 256)
+            quantize_hi(1, 256, 512)
+            odd_rows(2, 0, 256)
+            quantize_x(1, 0, 512)
+            for m in range(TILES):
+                hi_pass(1, m)
+                lo_pass(1, m)
+            subtract(2, 0, 256)
+            quantize_hi(2, 0, 256)
+            quantize_lo(2, 0, 256)
+            quantize_x(2, 0, 512)
+            for m in (0, 1):
+                hi_pass(2, m)
+                lo_pass(2, m)
+                finish(m)
+            mask_top(2, 256, 384)
+            subtract(2, 256, 384)
+            quantize_hi(2, 256, 384)
+            mask_top(2, 384, 512)
+            quantize_lo(2, 256, 384)
+            hi_pass(2, 2)
+            lo_pass(2, 2)
+            finish(2)
+            subtract(2, 384, 512)
+            quantize_hi(2, 384, 512)
+            hi_pass(2, 3)
+            quantize_lo(2, 384, 512)
+            lo_pass(2, 3)
+            finish(3, 2)

@@ -20,6 +20,9 @@ PACK = 4
 K_PASS = P * PACK
 PASSES = K // K_PASS
 TILES = M // P
+HALF = 256
+COPY_RUN = 4
+SUB_RUN = 4
 
 HI_WORD = -1048576
 HI_PAIR = -983056
@@ -36,208 +39,246 @@ def tile_mix_hilo_fm_silu_kernel(tc, w, x, b, out):
             t = keep.tile(shape, dtype, name=name, align_bytes=64)
             return t
 
-        def per_pass(name, shape, dtype):
-            return [keep_tile(name + str(g), shape, dtype) for g in range(PASSES)]
+        def per_unit(name, shape, dtype):
+            return {(g, h): keep_tile(name + str(g) + "h" + str(h), shape, dtype) for g in range(PASSES) for h in range(2)}
 
-        w_raw = per_pass("w_raw", [P, PACK, M], F32)
-        x_raw = per_pass("x_raw", [P, PACK, T], F32)
-        w_top = per_pass("w_top", [P, M, PACK], BF16)
-        w_even = per_pass("w_even", [P, 2, M], I32)
-        w_hi = per_pass("w_hi", [P, M, 2], I32)
-        w_lo = per_pass("w_lo", [P, M, PACK], BF16)
-        x_bf = per_pass("x_bf", [P, T, PACK], BF16)
-        hi_codes = per_pass("hi_codes", [P, M], U32)
-        hi_scales = per_pass("hi_scales", [P, M], U8)
-        lo_codes = per_pass("lo_codes", [P, M], U32)
-        lo_scales = per_pass("lo_scales", [P, M], U8)
-        x_codes = per_pass("x_codes", [P, T], U32)
-        x_scales = per_pass("x_scales", [P, T], U8)
-        acc = [psum.tile([P, T], F32, name="acc" + str(m)) for m in range(TILES)]
-        res = [keep_tile("res" + str(m), [P, T], F32) for m in range(TILES)]
+        w_top = per_unit("w_top", [P, HALF, PACK], BF16)
+        w_hi = per_unit("w_hi", [P, HALF, 2], I32)
+        w_lo = per_unit("w_lo", [P, HALF, PACK], BF16)
+        x_bf = per_unit("x_bf", [P, HALF, PACK], BF16)
+        hi_codes = per_unit("hi_codes", [P, HALF], U32)
+        hi_scales = per_unit("hi_scales", [P, HALF], U8)
+        lo_codes = per_unit("lo_codes", [P, HALF], U32)
+        lo_scales = per_unit("lo_scales", [P, HALF], U8)
+        x_codes = per_unit("x_codes", [P, HALF], U32)
+        x_scales = per_unit("x_scales", [P, HALF], U8)
+        w_even = keep_tile("w_even", [P, 2, HALF], I32)
+        acc = {(m, h): psum.tile([P, 2 * HALF], F32, name="acc" + str(m) + "h" + str(h)) for h in range(2) for m in range(TILES)}
+        res = {(m, h): keep_tile("res" + str(m) + "h" + str(h), [P, HALF], F32) for h in range(2) for m in range(TILES)}
 
         warm = keep_tile("warm", [P, 8], F32)
         b_rows = keep_tile("b_rows", [P, P], F32)
         b_cols = keep_tile("b_cols", [P, TILES], F32)
         ident = keep_tile("ident", [P, P], F32)
-        b_turn = psum.tile([P, P], F32, name="b_turn")
+        b_turn = acc[(TILES - 1, 1)]
 
-        def load(src, dst, g, c0, c1):
+        w_raw = {}
+        x_raw = {}
+
+        def load(src, dst, name, g, halves):
+            c0, c1 = halves[0] * HALF, (halves[-1] + 1) * HALF
+            raw = keep_tile(name + str(g) + "h" + str(halves[0]), [P, PACK, c1 - c0], F32)
             rows = src[g * K_PASS : (g + 1) * K_PASS, c0:c1]
-            nc.sync.dma_start(out=dst[g][:, :, c0:c1], in_=rows.rearrange("(p j) c -> p j c", j=PACK))
+            nc.sync.dma_start(out=raw[:], in_=rows.rearrange("(p j) c -> p j c", j=PACK))
+            for h in halves:
+                dst[(g, h)] = (raw, h * HALF - c0)
 
-        def grouped(t, g, c0, c1):
-            return t[g][:, c0:c1, :].rearrange("p (c i) t -> p c t i", i=4)
+        def grouped(t, u, c0, c1, i):
+            return t[u][:, c0:c1, :].rearrange("p (c i) t -> p c t i", i=i)
 
-        def by_row(t, g, c0, c1):
-            return t[g][:, :, c0:c1].rearrange("p t (c i) -> p c t i", i=4)
+        def by_row(raws, u, c0, c1, i):
+            raw, off = raws[u]
+            return raw[:, :, off + c0 : off + c1].rearrange("p t (c i) -> p c t i", i=i)
 
-        def top_halves(g, c0, c1):
-            halves = w_raw[g][:].bitcast(BF16)
+        def top_halves(u, c0=0, c1=HALF):
+            raw, off = w_raw[u]
+            halves = raw[:].bitcast(BF16)
             nc.scalar.copy(
-                out=grouped(w_top, g, c0, c1),
-                in_=halves[:, :, 2 * c0 + 1 : 2 * c1 : 2].rearrange("p t (c i) -> p c t i", i=4),
+                out=grouped(w_top, u, c0, c1, COPY_RUN),
+                in_=halves[:, :, 2 * (off + c0) + 1 : 2 * (off + c1) : 2].rearrange("p t (c i) -> p c t i", i=COPY_RUN),
             )
 
-        def mask_top(g, c0, c1):
+        def mask_top(u, c0=0, c1=HALF):
             nc.vector.tensor_scalar(
-                out=w_hi[g][:, c0:c1, :].rearrange("p c u -> p (c u)"),
-                in0=w_top[g][:, c0:c1, :].rearrange("p c t -> p (c t)").bitcast(I32),
+                out=w_hi[u][:, c0:c1, :].rearrange("p c u -> p (c u)"),
+                in0=w_top[u][:, c0:c1, :].rearrange("p c t -> p (c t)").bitcast(I32),
                 scalar1=HI_PAIR,
                 scalar2=None,
                 op0=ALU.bitwise_and,
             )
 
-        def even_rows(g, c0, c1):
-            words = w_raw[g][:].bitcast(I32)
+        def even_rows(u, c0=0, c1=HALF):
+            raw, off = w_raw[u]
+            words = raw[:].bitcast(I32)
             nc.vector.tensor_scalar(
-                out=w_even[g][:, :, c0:c1],
-                in0=words[:, 0:4:2, c0:c1],
+                out=w_even[:, :, c0:c1],
+                in0=words[:, 0:4:2, off + c0 : off + c1],
                 scalar1=16,
                 scalar2=HI_LOW_HALF,
                 op0=ALU.logical_shift_right,
                 op1=ALU.bitwise_and,
             )
 
-        def odd_rows(g, c0, c1):
-            words = w_raw[g][:].bitcast(I32)
+        def odd_rows(u, c0=0, c1=HALF):
+            raw, off = w_raw[u]
+            words = raw[:].bitcast(I32)
             nc.vector.scalar_tensor_tensor(
-                out=w_hi[g][:, c0:c1, :],
-                in0=words[:, 1:4:2, c0:c1].rearrange("p u c -> p c u"),
+                out=w_hi[u][:, c0:c1, :],
+                in0=words[:, 1:4:2, off + c0 : off + c1].rearrange("p u c -> p c u"),
                 scalar=HI_WORD,
-                in1=w_even[g][:, :, c0:c1].rearrange("p u c -> p c u"),
+                in1=w_even[:, :, c0:c1].rearrange("p u c -> p c u"),
                 op0=ALU.bitwise_and,
                 op1=ALU.bitwise_or,
             )
 
-        def subtract(g, c0, c1):
-            hi = w_hi[g][:].rearrange("p c u -> p (c u)").bitcast(BF16)[:, PACK * c0 : PACK * c1]
+        def hi_values(u, c0, c1):
+            return w_hi[u][:].rearrange("p c u -> p (c u)").bitcast(BF16)[:, PACK * c0 : PACK * c1]
+
+        def subtract(u, c0=0, c1=HALF):
             nc.vector.tensor_tensor(
-                out=grouped(w_lo, g, c0, c1),
-                in0=by_row(w_raw, g, c0, c1),
-                in1=hi.rearrange("p (c i t) -> p c t i", i=4, t=PACK),
+                out=grouped(w_lo, u, c0, c1, SUB_RUN),
+                in0=by_row(w_raw, u, c0, c1, SUB_RUN),
+                in1=hi_values(u, c0, c1).rearrange("p (c i t) -> p c t i", i=SUB_RUN, t=PACK),
                 op=ALU.subtract,
             )
 
-        def quantize(codes, scales, src, g, c0, c1):
-            nc.vector.quantize_mx(
-                out=codes[g][:, c0:c1].bitcast(FP8X4),
-                scales=scales[g][:, c0:c1],
-                in_=src,
-            )
+        def quantize(codes, scales, src, u, c0, c1):
+            nc.vector.quantize_mx(out=codes[u][:, c0:c1].bitcast(FP8X4), scales=scales[u][:, c0:c1], in_=src)
 
-        def quantize_hi(g, c0, c1):
-            src = w_hi[g][:].rearrange("p c u -> p (c u)").bitcast(BF16)[:, PACK * c0 : PACK * c1]
-            quantize(hi_codes, hi_scales, src, g, c0, c1)
+        def quantize_hi(u, c0=0, c1=HALF):
+            quantize(hi_codes, hi_scales, hi_values(u, c0, c1), u, c0, c1)
 
-        def quantize_lo(g, c0, c1):
-            quantize(lo_codes, lo_scales, w_lo[g][:].rearrange("p c t -> p (c t)")[:, PACK * c0 : PACK * c1], g, c0, c1)
+        def quantize_lo(u, c0=0, c1=HALF):
+            quantize(lo_codes, lo_scales, w_lo[u][:].rearrange("p c t -> p (c t)")[:, PACK * c0 : PACK * c1], u, c0, c1)
 
-        def quantize_x(g, c0, c1):
-            quantize(x_codes, x_scales, x_bf[g][:].rearrange("p c t -> p (c t)")[:, PACK * c0 : PACK * c1], g, c0, c1)
+        def quantize_x(u, c0=0, c1=HALF):
+            quantize(x_codes, x_scales, x_bf[u][:].rearrange("p c t -> p (c t)")[:, PACK * c0 : PACK * c1], u, c0, c1)
 
-        def round_x(engine_copy, g, c0, c1):
-            engine_copy(out=grouped(x_bf, g, c0, c1), in_=by_row(x_raw, g, c0, c1))
+        def round_x(engine_copy, u, c0=0, c1=HALF):
+            engine_copy(out=grouped(x_bf, u, c0, c1, COPY_RUN), in_=by_row(x_raw, u, c0, c1, COPY_RUN))
 
-        def multiply(codes, scales, g, m, start=False, stop=False):
-            cols = slice(m * P, (m + 1) * P)
+        def multiply(codes, scales, g, m, h, start=False, stop=False):
+            cols = slice((m % 2) * P, (m % 2 + 1) * P)
             nc.tensor.matmul_mx(
-                out=acc[m][:],
-                lhsT=codes[g][:, cols].bitcast(FP8X4),
-                lhsT_scale=scales[g][:, cols],
-                rhs=x_codes[g][:].bitcast(FP8X4),
-                rhs_scale=x_scales[g][:],
+                out=acc[(m, h)][:, 0:HALF],
+                lhsT=codes[(g, m // 2)][:, cols].bitcast(FP8X4),
+                lhsT_scale=scales[(g, m // 2)][:, cols],
+                rhs=x_codes[(g, h)][:].bitcast(FP8X4),
+                rhs_scale=x_scales[(g, h)][:],
                 start=start,
                 stop=stop,
             )
 
-        def hi_pass(g, m):
-            multiply(hi_codes, hi_scales, g, m, start=(g == 0))
+        def passes(g, h, ms=range(TILES)):
+            for m in ms:
+                multiply(hi_codes, hi_scales, g, m, h, start=(g == 0))
+                multiply(lo_codes, lo_scales, g, m, h, stop=(g == PASSES - 1))
 
-        def lo_pass(g, m):
-            multiply(lo_codes, lo_scales, g, m, stop=(g == PASSES - 1))
+        def hi_pass(g, m, h):
+            multiply(hi_codes, hi_scales, g, m, h, start=(g == 0))
 
-        def finish(m, parts=1):
-            for c in range(parts):
-                cols = slice(c * T // parts, (c + 1) * T // parts)
-                nc.scalar.activation(out=res[m][:, cols], in_=acc[m][:, cols], func=ACT.Silu, bias=b_cols[:, m : m + 1], scale=1.0)
-                nc.sync.dma_start(out=out[m * P : (m + 1) * P, cols], in_=res[m][:, cols])
+        def lo_pass(g, m, h):
+            multiply(lo_codes, lo_scales, g, m, h, stop=(g == PASSES - 1))
 
-        with tc.manual_schedule():
-            load(w, w_raw, 0, 0, 256)
-            load(w, w_raw, 0, 256, 512)
-            load(w, w_raw, 1, 0, 512)
-            load(x, x_raw, 0, 0, 512)
-            load(x, x_raw, 1, 0, 512)
-            load(w, w_raw, 2, 0, 256)
-            load(x, x_raw, 2, 0, 256)
-            load(x, x_raw, 2, 256, 512)
-            load(w, w_raw, 2, 256, 512)
+        def finish(m, h, queue=None):
+            nc.scalar.activation(out=res[(m, h)][:], in_=acc[(m, h)][:, 0:HALF], func=ACT.Silu, bias=b_cols[:, m : m + 1], scale=1.0)
+            (queue or nc.sync).dma_start(out=out[m * P : (m + 1) * P, h * HALF : (h + 1) * HALF], in_=res[(m, h)][:])
+
+        def constants():
             nc.vector.memset(b_rows[:], 0.0)
             nc.vector.memset(warm[:], 0.0)
             nc.scalar.dma_start(out=b_rows[0:TILES, :], in_=b.rearrange("(m p) -> m p", p=P))
             nc.scalar.activation(out=warm[:, 4:8], in_=warm[:, 0:4], func=ACT.Silu)
             make_identity(nc, ident[:])
-            nc.tensor.transpose(b_turn[:], b_rows[:], ident[:])
+            nc.tensor.transpose(b_turn[:, 0:P], b_rows[:], ident[:])
 
-            even_rows(0, 0, 256)
-            top_halves(0, 256, 512)
-            odd_rows(0, 0, 256)
-            subtract(0, 0, 256)
-            quantize_hi(0, 0, 256)
-            mask_top(0, 256, 512)
-            quantize_lo(0, 0, 256)
-            subtract(0, 256, 512)
-            quantize_hi(0, 256, 512)
-
-            top_halves(1, 0, 256)
-            top_halves(1, 256, 512)
-            mask_top(1, 0, 256)
-            quantize_lo(0, 256, 512)
-            quantize_hi(1, 0, 256)
-            subtract(1, 0, 256)
-            mask_top(1, 256, 512)
-            quantize_lo(1, 0, 256)
-            subtract(1, 256, 512)
-            round_x(nc.scalar.copy, 0, 0, 512)
+        with tc.manual_schedule():
+            load(w, w_raw, "w", 0, [0])
+            load(w, w_raw, "w", 0, [1])
+            load(w, w_raw, "w", 1, [0, 1])
+            load(x, x_raw, "x", 0, [0, 1])
+            load(w, w_raw, "w", 2, [0, 1])
+            load(x, x_raw, "x", 1, [0, 1])
+            load(x, x_raw, "x", 2, [0, 1])
+            constants()
+            S = nc.scalar.copy
+            V = nc.vector.tensor_copy
+            even_rows((0, 0), 0, 64)
+            even_rows((0, 0), 64, 128)
+            top_halves((0, 0), 128, 256)
+            odd_rows((0, 0), 0, 64)
+            odd_rows((0, 0), 64, 128)
+            subtract((0, 0), 0, 64)
+            subtract((0, 0), 64, 128)
+            mask_top((0, 0), 128, 256)
+            quantize_hi((0, 0), 0, 128)
+            quantize_lo((0, 0), 0, 128)
+            subtract((0, 0), 128, 256)
+            top_halves((0, 1), 0, 128)
+            top_halves((0, 1), 128, 256)
+            mask_top((0, 1), 0, 128)
+            quantize_hi((0, 0), 128, 256)
+            quantize_lo((0, 0), 128, 256)
+            subtract((0, 1), 0, 128)
+            mask_top((0, 1), 128, 256)
+            quantize_hi((0, 1), 0, 128)
+            quantize_lo((0, 1), 0, 128)
+            subtract((0, 1), 128, 256)
+            top_halves((1, 0), 0, 128)
+            top_halves((1, 0), 128, 256)
+            top_halves((1, 1))
+            mask_top((1, 0), 0, 128)
+            quantize_hi((0, 1), 128, 256)
+            quantize_lo((0, 1), 128, 256)
+            subtract((1, 0), 0, 128)
+            mask_top((1, 0), 128, 256)
+            quantize_hi((1, 0), 0, 128)
+            quantize_lo((1, 0), 0, 128)
+            subtract((1, 0), 128, 256)
+            mask_top((1, 1))
+            quantize_hi((1, 0), 128, 256)
+            quantize_lo((1, 0), 128, 256)
+            round_x(S, (0, 0))
+            round_x(S, (0, 1))
             nc.scalar.copy(out=b_cols[:], in_=b_turn[:, 0:TILES])
-            quantize_x(0, 0, 512)
-            for m in range(TILES):
-                hi_pass(0, m)
-                lo_pass(0, m)
-
-            round_x(nc.scalar.copy, 1, 0, 256)
-            round_x(nc.scalar.copy, 1, 256, 512)
-            round_x(nc.scalar.copy, 2, 0, 256)
-            round_x(nc.scalar.copy, 2, 256, 512)
-            top_halves(2, 256, 384)
-            top_halves(2, 384, 512)
-            quantize_lo(1, 256, 512)
-            even_rows(2, 0, 256)
-            quantize_hi(1, 256, 512)
-            odd_rows(2, 0, 256)
-            quantize_x(1, 0, 512)
-            for m in range(TILES):
-                hi_pass(1, m)
-                lo_pass(1, m)
-            subtract(2, 0, 256)
-            quantize_hi(2, 0, 256)
-            quantize_lo(2, 0, 256)
-            quantize_x(2, 0, 512)
-            for m in (0, 1):
-                hi_pass(2, m)
-                lo_pass(2, m)
-                finish(m)
-            mask_top(2, 256, 384)
-            subtract(2, 256, 384)
-            quantize_hi(2, 256, 384)
-            mask_top(2, 384, 512)
-            quantize_lo(2, 256, 384)
-            hi_pass(2, 2)
-            lo_pass(2, 2)
-            finish(2)
-            subtract(2, 384, 512)
-            quantize_hi(2, 384, 512)
-            hi_pass(2, 3)
-            quantize_lo(2, 384, 512)
-            lo_pass(2, 3)
-            finish(3, 2)
+            subtract((1, 1))
+            quantize_x((0, 0))
+            passes(0, 0)
+            quantize_hi((1, 1))
+            quantize_lo((1, 1))
+            top_halves((2, 0), 0, 128)
+            top_halves((2, 0), 128, 256)
+            top_halves((2, 1))
+            mask_top((2, 0), 0, 128)
+            quantize_x((0, 1))
+            passes(0, 1)
+            subtract((2, 0), 0, 128)
+            mask_top((2, 0), 128, 256)
+            round_x(V, (1, 1))
+            subtract((2, 0), 128, 256)
+            quantize_x((1, 1))
+            passes(1, 1)
+            quantize_hi((2, 0))
+            round_x(S, (1, 0))
+            mask_top((2, 1))
+            quantize_x((1, 0))
+            passes(1, 0)
+            quantize_lo((2, 0))
+            round_x(S, (2, 0))
+            round_x(V, (2, 1), 96, 256)
+            round_x(S, (2, 1), 0, 96)
+            quantize_hi((2, 1))
+            quantize_x((2, 0))
+            passes(2, 0, [0, 1])
+            finish(0, 0)
+            finish(1, 0)
+            subtract((2, 1), 0, 128)
+            quantize_x((2, 1))
+            hi_pass(2, 2, 0)
+            hi_pass(2, 3, 0)
+            passes(2, 1, [0, 1])
+            finish(0, 1)
+            finish(1, 1)
+            quantize_lo((2, 1), 0, 128)
+            subtract((2, 1), 128, 256)
+            hi_pass(2, 2, 1)
+            lo_pass(2, 2, 0)
+            lo_pass(2, 2, 1)
+            hi_pass(2, 3, 1)
+            finish(2, 0)
+            finish(2, 1)
+            quantize_lo((2, 1), 128, 256)
+            lo_pass(2, 3, 0)
+            lo_pass(2, 3, 1)
+            finish(3, 0)
+            finish(3, 1, nc.scalar)

@@ -22,7 +22,7 @@ PASSES = K // K_PASS
 TILES = M // P
 HALF = 256
 COPY_RUN = 4
-SUB_RUN = 4
+SUB_RUN = 2
 
 HI_WORD = -1048576
 HI_PAIR = -983056
@@ -65,23 +65,26 @@ def tile_mix_hilo_fm_silu_kernel(tc, w, x, b, out):
         w_raw = {}
         x_raw = {}
 
-        def load(src, dst, name, g, halves):
-            c0, c1 = halves[0] * HALF, (halves[-1] + 1) * HALF
-            raw = keep_tile(name + str(g) + "h" + str(halves[0]), [P, PACK, c1 - c0], F32)
-            rows = src[g * K_PASS : (g + 1) * K_PASS, c0:c1]
+        def load(src, dst, name, g, q0, q1):
+            raw = keep_tile(name + str(g) + "q" + str(q0), [P, PACK, (q1 - q0) * P], F32)
+            rows = src[g * K_PASS : (g + 1) * K_PASS, q0 * P : q1 * P]
             nc.sync.dma_start(out=raw[:], in_=rows.rearrange("(p j) c -> p j c", j=PACK))
-            for h in halves:
-                dst[(g, h)] = (raw, h * HALF - c0)
+            for q in range(q0, q1):
+                dst[(g, q)] = (raw, q0 * P)
+
+        def raw_of(raws, u, c0):
+            raw, first = raws[(u[0], (u[1] * HALF + c0) // P)]
+            return raw, u[1] * HALF - first
 
         def grouped(t, u, c0, c1, i):
             return t[u][:, c0:c1, :].rearrange("p (c i) t -> p c t i", i=i)
 
         def by_row(raws, u, c0, c1, i):
-            raw, off = raws[u]
+            raw, off = raw_of(raws, u, c0)
             return raw[:, :, off + c0 : off + c1].rearrange("p t (c i) -> p c t i", i=i)
 
         def top_halves(u, c0=0, c1=HALF):
-            raw, off = w_raw[u]
+            raw, off = raw_of(w_raw, u, c0)
             halves = raw[:].bitcast(BF16)
             nc.scalar.copy(
                 out=grouped(w_top, u, c0, c1, COPY_RUN),
@@ -98,7 +101,7 @@ def tile_mix_hilo_fm_silu_kernel(tc, w, x, b, out):
             )
 
         def even_rows(u, c0=0, c1=HALF):
-            raw, off = w_raw[u]
+            raw, off = raw_of(w_raw, u, c0)
             words = raw[:].bitcast(I32)
             nc.vector.tensor_scalar(
                 out=w_even[:, :, c0:c1],
@@ -110,7 +113,7 @@ def tile_mix_hilo_fm_silu_kernel(tc, w, x, b, out):
             )
 
         def odd_rows(u, c0=0, c1=HALF):
-            raw, off = w_raw[u]
+            raw, off = raw_of(w_raw, u, c0)
             words = raw[:].bitcast(I32)
             nc.vector.scalar_tensor_tensor(
                 out=w_hi[u][:, c0:c1, :],
@@ -183,13 +186,13 @@ def tile_mix_hilo_fm_silu_kernel(tc, w, x, b, out):
             nc.tensor.transpose(b_turn[:, 0:P], b_rows[:], ident[:])
 
         with tc.manual_schedule():
-            load(w, w_raw, "w", 0, [0])
-            load(w, w_raw, "w", 0, [1])
-            load(w, w_raw, "w", 1, [0, 1])
-            load(x, x_raw, "x", 0, [0, 1])
-            load(w, w_raw, "w", 2, [0, 1])
-            load(x, x_raw, "x", 1, [0, 1])
-            load(x, x_raw, "x", 2, [0, 1])
+            load(w, w_raw, "w", 0, 0, 2)
+            load(w, w_raw, "w", 0, 2, 4)
+            load(w, w_raw, "w", 1, 0, 4)
+            load(x, x_raw, "x", 0, 0, 4)
+            load(w, w_raw, "w", 2, 0, 4)
+            load(x, x_raw, "x", 1, 0, 4)
+            load(x, x_raw, "x", 2, 0, 4)
             constants()
             S = nc.scalar.copy
             V = nc.vector.tensor_copy

@@ -19,14 +19,18 @@ P = 128
 PACK = 4
 K_PASS = P * PACK
 PASSES = K // K_PASS
-TILES = M // P
-HALF = 256
-COPY_RUN = 4
-SUB_RUN = 2
+OUT_TILES = M // P
+W_TILES = PASSES * OUT_TILES
+HALF = T // 2
+LEFT, RIGHT = 0, 1
 
 HI_WORD = -1048576
 HI_PAIR = -983056
 HI_LOW_HALF = 0xFFF0
+
+COPY_RUN = 4
+SUB_RUN = 2
+SCALAR_SHARE = 96
 
 
 def tile_mix_hilo_fm_silu_kernel(tc, w, x, b, out):
@@ -35,253 +39,236 @@ def tile_mix_hilo_fm_silu_kernel(tc, w, x, b, out):
         keep = ctx.enter_context(tc.tile_pool(name="keep", bufs=1))
         psum = ctx.enter_context(tc.psum_pool(name="psum", bufs=1))
 
-        def keep_tile(name, shape, dtype):
-            t = keep.tile(shape, dtype, name=name, align_bytes=64)
-            return t
+        def sbuf(name, shape, dtype):
+            return keep.tile(shape, dtype, name=name, align_bytes=64)
 
-        def per_unit(name, shape, dtype):
-            return {(g, h): keep_tile(name + str(g) + "h" + str(h), shape, dtype) for g in range(PASSES) for h in range(2)}
+        def per_w_tile(name, shape, dtype):
+            return [sbuf(name + str(i), shape, dtype) for i in range(W_TILES)]
 
-        w_top = per_unit("w_top", [P, HALF, PACK], BF16)
-        w_hi = per_unit("w_hi", [P, HALF, 2], I32)
-        w_lo = per_unit("w_lo", [P, HALF, PACK], BF16)
-        x_bf = per_unit("x_bf", [P, HALF, PACK], BF16)
-        hi_codes = per_unit("hi_codes", [P, HALF], U32)
-        hi_scales = per_unit("hi_scales", [P, HALF], U8)
-        lo_codes = per_unit("lo_codes", [P, HALF], U32)
-        lo_scales = per_unit("lo_scales", [P, HALF], U8)
-        x_codes = per_unit("x_codes", [P, HALF], U32)
-        x_scales = per_unit("x_scales", [P, HALF], U8)
-        w_even = keep_tile("w_even", [P, 2, HALF], I32)
-        acc = {(m, h): psum.tile([P, 2 * HALF], F32, name="acc" + str(m) + "h" + str(h)) for h in range(2) for m in range(TILES)}
-        res = {(m, h): keep_tile("res" + str(m) + "h" + str(h), [P, HALF], F32) for h in range(2) for m in range(TILES)}
+        def per_x_half(name, shape, dtype):
+            return {(g, h): sbuf(name + str(2 * g + h), shape, dtype) for g in range(PASSES) for h in (LEFT, RIGHT)}
 
-        warm = keep_tile("warm", [P, 8], F32)
-        b_rows = keep_tile("b_rows", [P, P], F32)
-        b_cols = keep_tile("b_cols", [P, TILES], F32)
-        ident = keep_tile("ident", [P, P], F32)
-        b_turn = acc[(TILES - 1, 1)]
+        w_top = per_w_tile("w_top", [P, P * PACK], BF16)
+        w_hi = per_w_tile("w_hi", [P, P * PACK], BF16)
+        w_lo = per_w_tile("w_lo", [P, P * PACK], BF16)
+        hi_codes = per_w_tile("hi_codes", [P, P], U32)
+        hi_scales = per_w_tile("hi_scales", [P, P], U8)
+        lo_codes = per_w_tile("lo_codes", [P, P], U32)
+        lo_scales = per_w_tile("lo_scales", [P, P], U8)
+        x_bf = per_x_half("x_bf", [P, HALF * PACK], BF16)
+        x_codes = per_x_half("x_codes", [P, HALF], U32)
+        x_scales = per_x_half("x_scales", [P, HALF], U8)
+        banks = [(m, h) for h in (LEFT, RIGHT) for m in range(OUT_TILES)]
+        acc = {(m, h): psum.tile([P, 2 * HALF], F32, name="acc" + str(2 * m + h)) for m, h in banks}
+        res = {(m, h): sbuf("res" + str(2 * m + h), [P, HALF], F32) for m, h in banks}
+        b_rows = sbuf("b_rows", [P, P], F32)
+        b_cols = sbuf("b_cols", [P, OUT_TILES], F32)
+        ident = sbuf("ident", [P, P], F32)
+        warm = sbuf("warm", [P, 2], F32)
 
         w_raw = {}
         x_raw = {}
 
-        def load(src, dst, name, g, q0, q1):
-            raw = keep_tile(name + str(g) + "q" + str(q0), [P, PACK, (q1 - q0) * P], F32)
-            rows = src[g * K_PASS : (g + 1) * K_PASS, q0 * P : q1 * P]
+        def load(src, name, g, c0, c1):
+            raw = sbuf(name, [P, PACK, c1 - c0], F32)
+            rows = src[g * K_PASS : (g + 1) * K_PASS, c0:c1]
             nc.sync.dma_start(out=raw[:], in_=rows.rearrange("(p j) c -> p j c", j=PACK))
-            for q in range(q0, q1):
-                dst[(g, q)] = (raw, q0 * P)
+            return raw
 
-        def raw_of(raws, u, c0):
-            raw, first = raws[(u[0], (u[1] * HALF + c0) // P)]
-            return raw, u[1] * HALF - first
+        def load_w(g, m0, m1):
+            raw = load(w, "w_raw" + str(OUT_TILES * g + m0), g, m0 * P, m1 * P)
+            for m in range(m0, m1):
+                w_raw[OUT_TILES * g + m] = (raw, (m - m0) * P)
 
-        def grouped(t, u, c0, c1, i):
-            return t[u][:, c0:c1, :].rearrange("p (c i) t -> p c t i", i=i)
+        def load_x(g):
+            raw = load(x, "x_raw" + str(g), g, 0, T)
+            for h in (LEFT, RIGHT):
+                x_raw[(g, h)] = (raw, h * HALF)
 
-        def by_row(raws, u, c0, c1, i):
-            raw, off = raw_of(raws, u, c0)
-            return raw[:, :, off + c0 : off + c1].rearrange("p t (c i) -> p c t i", i=i)
+        def rows_walk(rows, run):
+            return rows.rearrange("p j (c i) -> p c j i", i=run)
 
-        def top_halves(u, c0=0, c1=HALF):
-            raw, off = raw_of(w_raw, u, c0)
-            halves = raw[:].bitcast(BF16)
-            nc.scalar.copy(
-                out=grouped(w_top, u, c0, c1, COPY_RUN),
-                in_=halves[:, :, 2 * (off + c0) + 1 : 2 * (off + c1) : 2].rearrange("p t (c i) -> p c t i", i=COPY_RUN),
+        def packed_walk(packed, c0, c1, run):
+            return packed[:, PACK * c0 : PACK * c1].rearrange("p (c i j) -> p c j i", i=run, j=PACK)
+
+        def copy_top(i):
+            raw, first = w_raw[i]
+            tops = raw[:].bitcast(BF16)[:, :, 2 * first + 1 : 2 * (first + P) : 2]
+            nc.scalar.copy(out=packed_walk(w_top[i], 0, P, COPY_RUN), in_=rows_walk(tops, COPY_RUN))
+
+        def mask_top(i):
+            nc.vector.tensor_scalar(
+                out=w_hi[i][:].bitcast(I32), in0=w_top[i][:].bitcast(I32), scalar1=HI_PAIR, scalar2=None, op0=ALU.bitwise_and
             )
 
-        def mask_top(u, c0=0, c1=HALF):
+        def shift_even_rows(i, c0, c1):
+            raw, first = w_raw[i]
             nc.vector.tensor_scalar(
-                out=w_hi[u][:, c0:c1, :].rearrange("p c u -> p (c u)"),
-                in0=w_top[u][:, c0:c1, :].rearrange("p c t -> p (c t)").bitcast(I32),
-                scalar1=HI_PAIR,
-                scalar2=None,
-                op0=ALU.bitwise_and,
-            )
-
-        def even_rows(u, c0=0, c1=HALF):
-            raw, off = raw_of(w_raw, u, c0)
-            words = raw[:].bitcast(I32)
-            nc.vector.tensor_scalar(
-                out=w_even[:, :, c0:c1],
-                in0=words[:, 0:4:2, off + c0 : off + c1],
+                out=w_top[i][:].bitcast(I32).rearrange("p (u c) -> p u c", u=2)[:, :, c0:c1],
+                in0=raw[:].bitcast(I32)[:, 0:PACK:2, first + c0 : first + c1],
                 scalar1=16,
                 scalar2=HI_LOW_HALF,
                 op0=ALU.logical_shift_right,
                 op1=ALU.bitwise_and,
             )
 
-        def odd_rows(u, c0=0, c1=HALF):
-            raw, off = raw_of(w_raw, u, c0)
-            words = raw[:].bitcast(I32)
+        def join_odd_rows(i, c0, c1):
+            raw, first = w_raw[i]
+            even = w_top[i][:].bitcast(I32).rearrange("p (u c) -> p u c", u=2)[:, :, c0:c1]
             nc.vector.scalar_tensor_tensor(
-                out=w_hi[u][:, c0:c1, :],
-                in0=words[:, 1:4:2, off + c0 : off + c1].rearrange("p u c -> p c u"),
+                out=w_hi[i][:].bitcast(I32)[:, 2 * c0 : 2 * c1].rearrange("p (c u) -> p c u", u=2),
+                in0=raw[:].bitcast(I32)[:, 1:PACK:2, first + c0 : first + c1].rearrange("p u c -> p c u"),
                 scalar=HI_WORD,
-                in1=w_even[:, :, c0:c1].rearrange("p u c -> p c u"),
+                in1=even.rearrange("p u c -> p c u"),
                 op0=ALU.bitwise_and,
                 op1=ALU.bitwise_or,
             )
 
-        def hi_values(u, c0, c1):
-            return w_hi[u][:].rearrange("p c u -> p (c u)").bitcast(BF16)[:, PACK * c0 : PACK * c1]
-
-        def subtract(u, c0=0, c1=HALF):
+        def subtract(i, c0=0, c1=P):
+            raw, first = w_raw[i]
             nc.vector.tensor_tensor(
-                out=grouped(w_lo, u, c0, c1, SUB_RUN),
-                in0=by_row(w_raw, u, c0, c1, SUB_RUN),
-                in1=hi_values(u, c0, c1).rearrange("p (c i t) -> p c t i", i=SUB_RUN, t=PACK),
+                out=packed_walk(w_lo[i], c0, c1, SUB_RUN),
+                in0=rows_walk(raw[:, :, first + c0 : first + c1], SUB_RUN),
+                in1=packed_walk(w_hi[i], c0, c1, SUB_RUN),
                 op=ALU.subtract,
             )
 
-        def quantize(codes, scales, src, u, c0, c1):
-            nc.vector.quantize_mx(out=codes[u][:, c0:c1].bitcast(FP8X4), scales=scales[u][:, c0:c1], in_=src)
+        def quantize_hi(i):
+            nc.vector.quantize_mx(out=hi_codes[i][:].bitcast(FP8X4), scales=hi_scales[i][:], in_=w_hi[i][:])
 
-        def quantize_hi(u, c0=0, c1=HALF):
-            quantize(hi_codes, hi_scales, hi_values(u, c0, c1), u, c0, c1)
+        def quantize_lo(i):
+            nc.vector.quantize_mx(out=lo_codes[i][:].bitcast(FP8X4), scales=lo_scales[i][:], in_=w_lo[i][:])
 
-        def quantize_lo(u, c0=0, c1=HALF):
-            quantize(lo_codes, lo_scales, w_lo[u][:].rearrange("p c t -> p (c t)")[:, PACK * c0 : PACK * c1], u, c0, c1)
+        def quantize_x(g, h):
+            nc.vector.quantize_mx(out=x_codes[(g, h)][:].bitcast(FP8X4), scales=x_scales[(g, h)][:], in_=x_bf[(g, h)][:])
 
-        def quantize_x(u, c0=0, c1=HALF):
-            quantize(x_codes, x_scales, x_bf[u][:].rearrange("p c t -> p (c t)")[:, PACK * c0 : PACK * c1], u, c0, c1)
+        def round_x(copy, g, h, c0=0, c1=HALF):
+            raw, first = x_raw[(g, h)]
+            copy(
+                out=packed_walk(x_bf[(g, h)], c0, c1, COPY_RUN),
+                in_=rows_walk(raw[:, :, first + c0 : first + c1], COPY_RUN),
+            )
 
-        def round_x(engine_copy, u, c0=0, c1=HALF):
-            engine_copy(out=grouped(x_bf, u, c0, c1, COPY_RUN), in_=by_row(x_raw, u, c0, c1, COPY_RUN))
+        def round_x_together(g, h):
+            round_x(nc.scalar.copy, g, h, 0, SCALAR_SHARE)
+            round_x(nc.vector.tensor_copy, g, h, SCALAR_SHARE, HALF)
 
-        def multiply(codes, scales, g, m, h, start=False, stop=False):
-            cols = slice((m % 2) * P, (m % 2 + 1) * P)
+        def multiply(codes, scales, g, m, h, start, stop):
             nc.tensor.matmul_mx(
                 out=acc[(m, h)][:, 0:HALF],
-                lhsT=codes[(g, m // 2)][:, cols].bitcast(FP8X4),
-                lhsT_scale=scales[(g, m // 2)][:, cols],
+                lhsT=codes[OUT_TILES * g + m][:].bitcast(FP8X4),
+                lhsT_scale=scales[OUT_TILES * g + m][:],
                 rhs=x_codes[(g, h)][:].bitcast(FP8X4),
                 rhs_scale=x_scales[(g, h)][:],
                 start=start,
                 stop=stop,
             )
 
-        def passes(g, h, ms=range(TILES)):
-            for m in ms:
-                multiply(hi_codes, hi_scales, g, m, h, start=(g == 0))
-                multiply(lo_codes, lo_scales, g, m, h, stop=(g == PASSES - 1))
-
         def hi_pass(g, m, h):
-            multiply(hi_codes, hi_scales, g, m, h, start=(g == 0))
+            multiply(hi_codes, hi_scales, g, m, h, start=(g == 0), stop=False)
 
         def lo_pass(g, m, h):
-            multiply(lo_codes, lo_scales, g, m, h, stop=(g == PASSES - 1))
+            multiply(lo_codes, lo_scales, g, m, h, start=False, stop=(g == PASSES - 1))
 
-        def finish(m, h, queue=None):
-            nc.scalar.activation(out=res[(m, h)][:], in_=acc[(m, h)][:, 0:HALF], func=ACT.Silu, bias=b_cols[:, m : m + 1], scale=1.0)
-            (queue or nc.sync).dma_start(out=out[m * P : (m + 1) * P, h * HALF : (h + 1) * HALF], in_=res[(m, h)][:])
+        def both_passes(g, h, out_tiles):
+            for m in out_tiles:
+                hi_pass(g, m, h)
+                lo_pass(g, m, h)
 
-        def constants():
+        def finish(m, h, queue):
+            nc.scalar.activation(
+                out=res[(m, h)][:], in_=acc[(m, h)][:, 0:HALF], func=ACT.Silu, bias=b_cols[:, m : m + 1], scale=1.0
+            )
+            queue.dma_start(out=out[m * P : (m + 1) * P, h * HALF : (h + 1) * HALF], in_=res[(m, h)][:])
+
+        all_tiles = range(OUT_TILES)
+        last = OUT_TILES - 1
+
+        with tc.manual_schedule():
+            load_w(0, 0, OUT_TILES // 2)
+            load_w(0, OUT_TILES // 2, OUT_TILES)
+            load_w(1, 0, OUT_TILES)
+            load_x(0)
+            load_w(2, 0, OUT_TILES)
+            load_x(1)
+            load_x(2)
+
+            b_turn = acc[(last, RIGHT)]
             nc.vector.memset(b_rows[:], 0.0)
             nc.vector.memset(warm[:], 0.0)
-            nc.scalar.dma_start(out=b_rows[0:TILES, :], in_=b.rearrange("(m p) -> m p", p=P))
-            nc.scalar.activation(out=warm[:, 4:8], in_=warm[:, 0:4], func=ACT.Silu)
+            nc.scalar.dma_start(out=b_rows[0:OUT_TILES, :], in_=b.rearrange("(m p) -> m p", p=P))
+            nc.scalar.activation(out=warm[:, 1:2], in_=warm[:, 0:1], func=ACT.Silu)
             make_identity(nc, ident[:])
             nc.tensor.transpose(b_turn[:, 0:P], b_rows[:], ident[:])
 
-        with tc.manual_schedule():
-            load(w, w_raw, "w", 0, 0, 2)
-            load(w, w_raw, "w", 0, 2, 4)
-            load(w, w_raw, "w", 1, 0, 4)
-            load(x, x_raw, "x", 0, 0, 4)
-            load(w, w_raw, "w", 2, 0, 4)
-            load(x, x_raw, "x", 1, 0, 4)
-            load(x, x_raw, "x", 2, 0, 4)
-            constants()
-            S = nc.scalar.copy
-            V = nc.vector.tensor_copy
-            even_rows((0, 0), 0, 64)
-            even_rows((0, 0), 64, 128)
-            top_halves((0, 0), 128, 256)
-            odd_rows((0, 0), 0, 64)
-            odd_rows((0, 0), 64, 128)
-            subtract((0, 0), 0, 64)
-            subtract((0, 0), 64, 128)
-            mask_top((0, 0), 128, 256)
-            quantize_hi((0, 0), 0, 128)
-            quantize_lo((0, 0), 0, 128)
-            subtract((0, 0), 128, 256)
-            top_halves((0, 1), 0, 128)
-            top_halves((0, 1), 128, 256)
-            mask_top((0, 1), 0, 128)
-            quantize_hi((0, 0), 128, 256)
-            quantize_lo((0, 0), 128, 256)
-            subtract((0, 1), 0, 128)
-            mask_top((0, 1), 128, 256)
-            quantize_hi((0, 1), 0, 128)
-            quantize_lo((0, 1), 0, 128)
-            subtract((0, 1), 128, 256)
-            top_halves((1, 0), 0, 128)
-            top_halves((1, 0), 128, 256)
-            top_halves((1, 1))
-            mask_top((1, 0), 0, 128)
-            quantize_hi((0, 1), 128, 256)
-            quantize_lo((0, 1), 128, 256)
-            subtract((1, 0), 0, 128)
-            mask_top((1, 0), 128, 256)
-            quantize_hi((1, 0), 0, 128)
-            quantize_lo((1, 0), 0, 128)
-            subtract((1, 0), 128, 256)
-            mask_top((1, 1))
-            quantize_hi((1, 0), 128, 256)
-            quantize_lo((1, 0), 128, 256)
-            round_x(S, (0, 0))
-            round_x(S, (0, 1))
-            nc.scalar.copy(out=b_cols[:], in_=b_turn[:, 0:TILES])
-            subtract((1, 1))
-            quantize_x((0, 0))
-            passes(0, 0)
-            quantize_hi((1, 1))
-            quantize_lo((1, 1))
-            top_halves((2, 0), 0, 128)
-            top_halves((2, 0), 128, 256)
-            top_halves((2, 1))
-            mask_top((2, 0), 0, 128)
-            quantize_x((0, 1))
-            passes(0, 1)
-            subtract((2, 0), 0, 128)
-            mask_top((2, 0), 128, 256)
-            round_x(V, (1, 1))
-            subtract((2, 0), 128, 256)
-            quantize_x((1, 1))
-            passes(1, 1)
-            quantize_hi((2, 0))
-            round_x(S, (1, 0))
-            mask_top((2, 1))
-            quantize_x((1, 0))
-            passes(1, 0)
-            quantize_lo((2, 0))
-            round_x(S, (2, 0))
-            round_x(V, (2, 1), 96, 256)
-            round_x(S, (2, 1), 0, 96)
-            quantize_hi((2, 1))
-            quantize_x((2, 0))
-            passes(2, 0, [0, 1])
-            finish(0, 0)
-            finish(1, 0)
-            subtract((2, 1), 0, 128)
-            quantize_x((2, 1))
-            hi_pass(2, 2, 0)
-            hi_pass(2, 3, 0)
-            passes(2, 1, [0, 1])
-            finish(0, 1)
-            finish(1, 1)
-            quantize_lo((2, 1), 0, 128)
-            subtract((2, 1), 128, 256)
-            hi_pass(2, 2, 1)
-            lo_pass(2, 2, 0)
-            lo_pass(2, 2, 1)
-            hi_pass(2, 3, 1)
-            finish(2, 0)
-            finish(2, 1)
-            quantize_lo((2, 1), 128, 256)
-            lo_pass(2, 3, 0)
-            lo_pass(2, 3, 1)
-            finish(3, 0)
-            finish(3, 1, nc.scalar)
+            for i in range(1, 2 * OUT_TILES):
+                copy_top(i)
+            round_x(nc.scalar.copy, 0, LEFT)
+            round_x(nc.scalar.copy, 0, RIGHT)
+            nc.scalar.copy(out=b_cols[:], in_=b_turn[:, 0:OUT_TILES])
+            for i in range(2 * OUT_TILES, W_TILES - 1):
+                copy_top(i)
+
+            first_halves = ((0, P // 2), (P // 2, P))
+            for step in (shift_even_rows, join_odd_rows, subtract):
+                for c0, c1 in first_halves:
+                    step(0, c0, c1)
+            mask_top(1)
+            quantize_hi(0)
+            quantize_lo(0)
+
+            for i in range(1, 2 * OUT_TILES):
+                if i == 2 * OUT_TILES - 1:
+                    quantize_x(0, LEFT)
+                    both_passes(0, LEFT, all_tiles)
+                subtract(i)
+                if i == 2 * OUT_TILES - 1:
+                    quantize_x(0, RIGHT)
+                    both_passes(0, RIGHT, all_tiles)
+                mask_top(i + 1)
+                quantize_hi(i)
+                quantize_lo(i)
+
+            tile_0, tile_1, tile_2, tile_3 = range(2 * OUT_TILES, W_TILES)
+            subtract(tile_0)
+            mask_top(tile_1)
+            round_x_together(1, LEFT)
+            quantize_hi(tile_0)
+            quantize_lo(tile_0)
+            quantize_x(1, LEFT)
+            both_passes(1, LEFT, all_tiles)
+            round_x(nc.scalar.copy, 1, RIGHT)
+            copy_top(tile_3)
+
+            subtract(tile_1)
+            mask_top(tile_2)
+            quantize_hi(tile_1)
+            quantize_x(1, RIGHT)
+            both_passes(1, RIGHT, all_tiles)
+            round_x_together(2, LEFT)
+            quantize_lo(tile_1)
+            quantize_x(2, LEFT)
+            both_passes(2, LEFT, range(last - 1))
+            round_x(nc.scalar.copy, 2, RIGHT)
+
+            subtract(tile_2)
+            mask_top(tile_3)
+            quantize_hi(tile_2)
+            quantize_lo(tile_2)
+            both_passes(2, LEFT, [last - 1])
+            quantize_x(2, RIGHT)
+            both_passes(2, RIGHT, range(last))
+
+            subtract(tile_3)
+            quantize_hi(tile_3)
+            for h in (LEFT, RIGHT):
+                hi_pass(2, last, h)
+            quantize_lo(tile_3)
+            for h in (LEFT, RIGHT):
+                lo_pass(2, last, h)
+
+            for h in (LEFT, RIGHT):
+                for m in range(last):
+                    finish(m, h, nc.sync)
+            finish(last, LEFT, nc.sync)
+            finish(last, RIGHT, nc.scalar)

@@ -23,14 +23,14 @@ OUT_TILES = M // P
 W_TILES = PASSES * OUT_TILES
 HALF = T // 2
 LEFT, RIGHT = 0, 1
+HI, LO = 0, 1
 
 HI_WORD = -1048576
 HI_PAIR = -983056
-HI_LOW_HALF = 0xFFF0
-
 COPY_RUN = 4
 SUB_RUN = 2
 SCALAR_SHARE = 96
+GROUPS = ((0,), (1,), (2,), (3,), (4,), (5,), (6,), (7,), (8,), (9,), (10,), (11,))
 
 
 def tile_mix_hilo_fm_silu_kernel(tc, w, x, b, out):
@@ -42,25 +42,24 @@ def tile_mix_hilo_fm_silu_kernel(tc, w, x, b, out):
         def sbuf(name, shape, dtype):
             return keep.tile(shape, dtype, name=name, align_bytes=64)
 
-        def per_w_tile(name, shape, dtype):
-            return [sbuf(name + str(i), shape, dtype) for i in range(W_TILES)]
+        def per_group(name, width, dtype):
+            return {grp[0]: sbuf(name + str(grp[0]), [P, width * len(grp)], dtype) for grp in GROUPS}
 
         def per_x_half(name, shape, dtype):
             return {(g, h): sbuf(name + str(2 * g + h), shape, dtype) for g in range(PASSES) for h in (LEFT, RIGHT)}
 
-        w_top = per_w_tile("w_top", [P, P * PACK], BF16)
-        w_hi = per_w_tile("w_hi", [P, P * PACK], BF16)
-        w_lo = per_w_tile("w_lo", [P, P * PACK], BF16)
-        hi_codes = per_w_tile("hi_codes", [P, P], U32)
-        hi_scales = per_w_tile("hi_scales", [P, P], U8)
-        lo_codes = per_w_tile("lo_codes", [P, P], U32)
-        lo_scales = per_w_tile("lo_scales", [P, P], U8)
+        group_of = {i: grp for grp in GROUPS for i in grp}
+        w_top = per_group("w_top", P * PACK, BF16)
+        w_parts = per_group("w_parts", 2 * P * PACK, BF16)
+        w_codes = per_group("w_codes", 2 * P, U32)
+        w_scales = per_group("w_scales", 2 * P, U8)
         x_bf = per_x_half("x_bf", [P, HALF * PACK], BF16)
         x_codes = per_x_half("x_codes", [P, HALF], U32)
         x_scales = per_x_half("x_scales", [P, HALF], U8)
         banks = [(m, h) for h in (LEFT, RIGHT) for m in range(OUT_TILES)]
         acc = {(m, h): psum.tile([P, 2 * HALF], F32, name="acc" + str(2 * m + h)) for m, h in banks}
         res = {(m, h): sbuf("res" + str(2 * m + h), [P, HALF], F32) for m, h in banks}
+        hi_words = sbuf("hi_words", [P, PACK, P], F32)
         b_rows = sbuf("b_rows", [P, P], F32)
         b_cols = sbuf("b_cols", [P, OUT_TILES], F32)
         ident = sbuf("ident", [P, P], F32)
@@ -85,62 +84,82 @@ def tile_mix_hilo_fm_silu_kernel(tc, w, x, b, out):
             for h in (LEFT, RIGHT):
                 x_raw[(g, h)] = (raw, h * HALF)
 
+        def load_x_half(g, h):
+            x_raw[(g, h)] = (load(x, "x_half" + str(2 * g + h), g, h * HALF, (h + 1) * HALF), 0)
+
         def rows_walk(rows, run):
             return rows.rearrange("p j (c i) -> p c j i", i=run)
 
         def packed_walk(packed, c0, c1, run):
             return packed[:, PACK * c0 : PACK * c1].rearrange("p (c i j) -> p c j i", i=run, j=PACK)
 
-        def copy_top(i):
-            raw, first = w_raw[i]
-            tops = raw[:].bitcast(BF16)[:, :, 2 * first + 1 : 2 * (first + P) : 2]
-            nc.scalar.copy(out=packed_walk(w_top[i], 0, P, COPY_RUN), in_=rows_walk(tops, COPY_RUN))
+        def width(i):
+            return P * len(group_of[i])
 
-        def mask_top(i):
+        def part(i, which):
+            return w_parts[i][:, which * PACK * width(i) : (which + 1) * PACK * width(i)]
+
+        def copy_top(i, c0=0, c1=None):
+            raw, first = w_raw[i]
+            c1 = width(i) if c1 is None else c1
+            tops = raw[:].bitcast(BF16)[:, :, 2 * (first + c0) + 1 : 2 * (first + c1) : 2]
+            nc.scalar.copy(out=packed_walk(w_top[i], c0, c1, COPY_RUN), in_=rows_walk(tops, COPY_RUN))
+
+        def mask_top(i, c0=0, c1=None):
+            c1 = width(i) if c1 is None else c1
             nc.vector.tensor_scalar(
-                out=w_hi[i][:].bitcast(I32), in0=w_top[i][:].bitcast(I32), scalar1=HI_PAIR, scalar2=None, op0=ALU.bitwise_and
-            )
-
-        def shift_even_rows(i, c0, c1):
-            raw, first = w_raw[i]
-            nc.vector.tensor_scalar(
-                out=w_top[i][:].bitcast(I32).rearrange("p (u c) -> p u c", u=2)[:, :, c0:c1],
-                in0=raw[:].bitcast(I32)[:, 0:PACK:2, first + c0 : first + c1],
-                scalar1=16,
-                scalar2=HI_LOW_HALF,
-                op0=ALU.logical_shift_right,
-                op1=ALU.bitwise_and,
-            )
-
-        def join_odd_rows(i, c0, c1):
-            raw, first = w_raw[i]
-            even = w_top[i][:].bitcast(I32).rearrange("p (u c) -> p u c", u=2)[:, :, c0:c1]
-            nc.vector.scalar_tensor_tensor(
-                out=w_hi[i][:].bitcast(I32)[:, 2 * c0 : 2 * c1].rearrange("p (c u) -> p c u", u=2),
-                in0=raw[:].bitcast(I32)[:, 1:PACK:2, first + c0 : first + c1].rearrange("p u c -> p c u"),
-                scalar=HI_WORD,
-                in1=even.rearrange("p u c -> p c u"),
+                out=part(i, HI)[:, PACK * c0 : PACK * c1].bitcast(I32),
+                in0=w_top[i][:, PACK * c0 : PACK * c1].bitcast(I32),
+                scalar1=HI_PAIR,
+                scalar2=None,
                 op0=ALU.bitwise_and,
-                op1=ALU.bitwise_or,
             )
 
-        def subtract(i, c0=0, c1=P):
-            raw, first = w_raw[i]
+        def mask_words(c0, c1):
+            raw, first = w_raw[0]
+            nc.vector.tensor_scalar(
+                out=hi_words[:].bitcast(I32)[:, :, c0:c1],
+                in0=raw[:].bitcast(I32)[:, :, first + c0 : first + c1],
+                scalar1=HI_WORD,
+                scalar2=None,
+                op0=ALU.bitwise_and,
+            )
+
+        def subtract_words(c0, c1):
+            raw, first = w_raw[0]
             nc.vector.tensor_tensor(
-                out=packed_walk(w_lo[i], c0, c1, SUB_RUN),
+                out=packed_walk(part(0, LO), c0, c1, SUB_RUN),
                 in0=rows_walk(raw[:, :, first + c0 : first + c1], SUB_RUN),
-                in1=packed_walk(w_hi[i], c0, c1, SUB_RUN),
+                in1=rows_walk(hi_words[:, :, c0:c1], SUB_RUN),
                 op=ALU.subtract,
             )
 
-        def quantize_hi(i):
-            nc.vector.quantize_mx(out=hi_codes[i][:].bitcast(FP8X4), scales=hi_scales[i][:], in_=w_hi[i][:])
+        def copy_hi():
+            nc.scalar.copy(out=packed_walk(part(0, HI), 0, P, COPY_RUN), in_=rows_walk(hi_words[:], COPY_RUN))
 
-        def quantize_lo(i):
-            nc.vector.quantize_mx(out=lo_codes[i][:].bitcast(FP8X4), scales=lo_scales[i][:], in_=w_lo[i][:])
+        def subtract(i, c0=0, c1=None):
+            raw, first = w_raw[i]
+            c1 = width(i) if c1 is None else c1
+            nc.vector.tensor_tensor(
+                out=packed_walk(part(i, LO), c0, c1, SUB_RUN),
+                in0=rows_walk(raw[:, :, first + c0 : first + c1], SUB_RUN),
+                in1=packed_walk(part(i, HI), c0, c1, SUB_RUN),
+                op=ALU.subtract,
+            )
 
-        def quantize_x(g, h):
-            nc.vector.quantize_mx(out=x_codes[(g, h)][:].bitcast(FP8X4), scales=x_scales[(g, h)][:], in_=x_bf[(g, h)][:])
+        def quantize_part(i, which):
+            cols = slice(which * width(i), (which + 1) * width(i))
+            nc.vector.quantize_mx(out=w_codes[i][:, cols].bitcast(FP8X4), scales=w_scales[i][:, cols], in_=part(i, which))
+
+        def quantize_w(i):
+            nc.vector.quantize_mx(out=w_codes[i][:].bitcast(FP8X4), scales=w_scales[i][:], in_=w_parts[i][:])
+
+        def quantize_x(g, h, c0=0, c1=HALF):
+            nc.vector.quantize_mx(
+                out=x_codes[(g, h)][:, c0:c1].bitcast(FP8X4),
+                scales=x_scales[(g, h)][:, c0:c1],
+                in_=x_bf[(g, h)][:, PACK * c0 : PACK * c1],
+            )
 
         def round_x(copy, g, h, c0=0, c1=HALF):
             raw, first = x_raw[(g, h)]
@@ -149,31 +168,28 @@ def tile_mix_hilo_fm_silu_kernel(tc, w, x, b, out):
                 in_=rows_walk(raw[:, :, first + c0 : first + c1], COPY_RUN),
             )
 
-        def round_x_together(g, h):
-            round_x(nc.scalar.copy, g, h, 0, SCALAR_SHARE)
-            round_x(nc.vector.tensor_copy, g, h, SCALAR_SHARE, HALF)
+        def round_x_together(g, h, share=SCALAR_SHARE):
+            round_x(nc.scalar.copy, g, h, 0, share)
+            round_x(nc.vector.tensor_copy, g, h, share, HALF)
 
-        def multiply(codes, scales, g, m, h, start, stop):
+        def multiply(which, g, m, h, c0=0, c1=HALF):
+            i = OUT_TILES * g + m
+            lead = group_of[i][0]
+            first = which * width(i) + (i - lead) * P
             nc.tensor.matmul_mx(
-                out=acc[(m, h)][:, 0:HALF],
-                lhsT=codes[OUT_TILES * g + m][:].bitcast(FP8X4),
-                lhsT_scale=scales[OUT_TILES * g + m][:],
-                rhs=x_codes[(g, h)][:].bitcast(FP8X4),
-                rhs_scale=x_scales[(g, h)][:],
-                start=start,
-                stop=stop,
+                out=acc[(m, h)][:, c0:c1],
+                lhsT=w_codes[lead][:, first : first + P].bitcast(FP8X4),
+                lhsT_scale=w_scales[lead][:, first : first + P],
+                rhs=x_codes[(g, h)][:, c0:c1].bitcast(FP8X4),
+                rhs_scale=x_scales[(g, h)][:, c0:c1],
+                start=(g == 0 and which == HI and c0 == 0),
+                stop=(g == PASSES - 1 and which == LO and c1 == HALF),
             )
 
-        def hi_pass(g, m, h):
-            multiply(hi_codes, hi_scales, g, m, h, start=(g == 0), stop=False)
-
-        def lo_pass(g, m, h):
-            multiply(lo_codes, lo_scales, g, m, h, start=False, stop=(g == PASSES - 1))
-
-        def both_passes(g, h, out_tiles):
+        def both_passes(g, h, out_tiles, c0=0, c1=HALF):
             for m in out_tiles:
-                hi_pass(g, m, h)
-                lo_pass(g, m, h)
+                multiply(HI, g, m, h, c0, c1)
+                multiply(LO, g, m, h, c0, c1)
 
         def finish(m, h, queue):
             nc.scalar.activation(
@@ -185,88 +201,97 @@ def tile_mix_hilo_fm_silu_kernel(tc, w, x, b, out):
         last = OUT_TILES - 1
 
         with tc.manual_schedule():
-            load_w(0, 0, OUT_TILES // 2)
-            load_w(0, OUT_TILES // 2, OUT_TILES)
-            load_w(1, 0, OUT_TILES)
+            load_w(0, 0, 2)
+            load_w(0, 2, 4)
+            load_w(1, 0, 4)
             load_x(0)
-            load_w(2, 0, OUT_TILES)
+            load_w(2, 0, 4)
             load_x(1)
-            load_x(2)
+            load_x_half(2, LEFT)
 
             b_turn = acc[(last, RIGHT)]
             nc.vector.memset(b_rows[:], 0.0)
             nc.vector.memset(warm[:], 0.0)
             nc.scalar.dma_start(out=b_rows[0:OUT_TILES, :], in_=b.rearrange("(m p) -> m p", p=P))
+            load_x_half(2, RIGHT)
             nc.scalar.activation(out=warm[:, 1:2], in_=warm[:, 0:1], func=ACT.Silu)
             make_identity(nc, ident[:])
             nc.tensor.transpose(b_turn[:, 0:P], b_rows[:], ident[:])
 
-            for i in range(1, 2 * OUT_TILES):
+            copy_top(1)
+            mask_words(0, 64)
+            mask_words(64, P)
+            subtract_words(0, 64)
+            subtract_words(64, P)
+            copy_hi()
+            for i in range(2, 8):
                 copy_top(i)
             round_x(nc.scalar.copy, 0, LEFT)
             round_x(nc.scalar.copy, 0, RIGHT)
             nc.scalar.copy(out=b_cols[:], in_=b_turn[:, 0:OUT_TILES])
-            for i in range(2 * OUT_TILES, W_TILES - 1):
+            for i in range(8, 12):
                 copy_top(i)
-
-            first_halves = ((0, P // 2), (P // 2, P))
-            for step in (shift_even_rows, join_odd_rows, subtract):
-                for c0, c1 in first_halves:
-                    step(0, c0, c1)
             mask_top(1)
-            quantize_hi(0)
-            quantize_lo(0)
-
-            for i in range(1, 2 * OUT_TILES):
-                if i == 2 * OUT_TILES - 1:
-                    quantize_x(0, LEFT)
-                    both_passes(0, LEFT, all_tiles)
-                subtract(i)
-                if i == 2 * OUT_TILES - 1:
-                    quantize_x(0, RIGHT)
-                    both_passes(0, RIGHT, all_tiles)
-                mask_top(i + 1)
-                quantize_hi(i)
-                quantize_lo(i)
-
-            tile_0, tile_1, tile_2, tile_3 = range(2 * OUT_TILES, W_TILES)
-            subtract(tile_0)
-            mask_top(tile_1)
-            round_x_together(1, LEFT)
-            quantize_hi(tile_0)
-            quantize_lo(tile_0)
+            quantize_part(0, LO)
+            subtract(1)
+            quantize_part(0, HI)
+            quantize_part(1, HI)
+            mask_top(2)
+            quantize_part(1, LO)
+            subtract(2)
+            mask_top(3)
+            quantize_part(2, HI)
+            quantize_part(2, LO)
+            subtract(3)
+            quantize_part(3, HI)
+            mask_top(4)
+            quantize_part(3, LO)
+            subtract(4)
+            mask_top(5)
+            mask_top(6)
+            subtract(5)
+            quantize_w(4)
+            subtract(6)
+            quantize_x(0, LEFT)
+            both_passes(0, LEFT, all_tiles)
+            mask_top(7)
+            quantize_w(5)
+            subtract(7)
+            quantize_x(0, RIGHT)
+            both_passes(0, RIGHT, all_tiles)
+            mask_top(8)
+            quantize_w(6)
+            subtract(8)
+            mask_top(9)
+            quantize_w(7)
+            round_x_together(1, LEFT, 96)
+            round_x(nc.scalar.copy, 1, RIGHT)
+            mask_top(10)
+            quantize_w(8)
             quantize_x(1, LEFT)
             both_passes(1, LEFT, all_tiles)
-            round_x(nc.scalar.copy, 1, RIGHT)
-            copy_top(tile_3)
-
-            subtract(tile_1)
-            mask_top(tile_2)
-            quantize_hi(tile_1)
+            subtract(9)
+            round_x(nc.scalar.copy, 2, LEFT)
+            mask_top(11)
             quantize_x(1, RIGHT)
             both_passes(1, RIGHT, all_tiles)
-            round_x_together(2, LEFT)
-            quantize_lo(tile_1)
+            quantize_w(9)
+            subtract(10)
             quantize_x(2, LEFT)
-            both_passes(2, LEFT, range(last - 1))
-            round_x(nc.scalar.copy, 2, RIGHT)
-
-            subtract(tile_2)
-            mask_top(tile_3)
-            quantize_hi(tile_2)
-            quantize_lo(tile_2)
-            both_passes(2, LEFT, [last - 1])
+            both_passes(2, LEFT, range(2))
+            round_x_together(2, RIGHT, 192)
+            quantize_w(10)
+            both_passes(2, LEFT, [2])
+            subtract(11, 0, 64)
             quantize_x(2, RIGHT)
             both_passes(2, RIGHT, range(last))
-
-            subtract(tile_3)
-            quantize_hi(tile_3)
+            subtract(11, 64, P)
+            quantize_part(11, HI)
             for h in (LEFT, RIGHT):
-                hi_pass(2, last, h)
-            quantize_lo(tile_3)
+                multiply(HI, 2, last, h)
+            quantize_part(11, LO)
             for h in (LEFT, RIGHT):
-                lo_pass(2, last, h)
-
+                multiply(LO, 2, last, h)
             for h in (LEFT, RIGHT):
                 for m in range(last):
                     finish(m, h, nc.sync)

@@ -84,9 +84,6 @@ def tile_mix_hilo_fm_silu_kernel(tc, w, x, b, out):
             for h in (LEFT, RIGHT):
                 x_raw[(g, h)] = (raw, h * HALF)
 
-        def load_x_half(g, h):
-            x_raw[(g, h)] = (load(x, "x_half" + str(2 * g + h), g, h * HALF, (h + 1) * HALF), 0)
-
         def rows_walk(rows, run):
             return rows.rearrange("p j (c i) -> p c j i", i=run)
 
@@ -103,7 +100,7 @@ def tile_mix_hilo_fm_silu_kernel(tc, w, x, b, out):
             raw, first = w_raw[i]
             c1 = width(i) if c1 is None else c1
             tops = raw[:].bitcast(BF16)[:, :, 2 * (first + c0) + 1 : 2 * (first + c1) : 2]
-            nc.scalar.copy(out=packed_walk(w_top[i], c0, c1, COPY_RUN), in_=rows_walk(tops, COPY_RUN))
+            nc.scalar.activation(out=packed_walk(w_top[i], c0, c1, COPY_RUN), in_=rows_walk(tops, COPY_RUN), func=ACT.Copy)
 
         def mask_top(i, c0=0, c1=None):
             c1 = width(i) if c1 is None else c1
@@ -201,19 +198,18 @@ def tile_mix_hilo_fm_silu_kernel(tc, w, x, b, out):
         last = OUT_TILES - 1
 
         with tc.manual_schedule():
-            load_w(0, 0, 2)
-            load_w(0, 2, 4)
-            load_w(1, 0, 4)
+            load_w(0, 0, OUT_TILES // 2)
+            load_w(0, OUT_TILES // 2, OUT_TILES)
+            load_w(1, 0, OUT_TILES)
             load_x(0)
-            load_w(2, 0, 4)
+            load_w(2, 0, OUT_TILES)
             load_x(1)
-            load_x_half(2, LEFT)
+            load_x(2)
 
             b_turn = acc[(last, RIGHT)]
             nc.vector.memset(b_rows[:], 0.0)
             nc.vector.memset(warm[:], 0.0)
             nc.scalar.dma_start(out=b_rows[0:OUT_TILES, :], in_=b.rearrange("(m p) -> m p", p=P))
-            load_x_half(2, RIGHT)
             nc.scalar.activation(out=warm[:, 1:2], in_=warm[:, 0:1], func=ACT.Silu)
             make_identity(nc, ident[:])
             nc.tensor.transpose(b_turn[:, 0:P], b_rows[:], ident[:])
@@ -271,21 +267,21 @@ def tile_mix_hilo_fm_silu_kernel(tc, w, x, b, out):
             quantize_x(1, LEFT)
             both_passes(1, LEFT, all_tiles)
             subtract(9)
-            round_x(nc.scalar.copy, 2, LEFT)
             mask_top(11)
             quantize_x(1, RIGHT)
             both_passes(1, RIGHT, all_tiles)
+            round_x_together(2, LEFT, 96)
             quantize_w(9)
-            subtract(10)
             quantize_x(2, LEFT)
             both_passes(2, LEFT, range(2))
-            round_x_together(2, RIGHT, 192)
-            quantize_w(10)
+            round_x(nc.scalar.copy, 2, RIGHT)
+            subtract(10)
+            quantize_part(10, HI)
+            quantize_part(10, LO)
             both_passes(2, LEFT, [2])
-            subtract(11, 0, 64)
             quantize_x(2, RIGHT)
             both_passes(2, RIGHT, range(last))
-            subtract(11, 64, P)
+            subtract(11)
             quantize_part(11, HI)
             for h in (LEFT, RIGHT):
                 multiply(HI, 2, last, h)

@@ -158,16 +158,16 @@ def tile_mix_hilo_fm_silu_kernel(tc, w, x, b, out):
                 in_=x_bf[(g, h)][:, PACK * c0 : PACK * c1],
             )
 
-        def round_x(copy, g, h, c0=0, c1=HALF):
+        def round_x(copy, g, h, c0=0, c1=HALF, run=COPY_RUN):
             raw, first = x_raw[(g, h)]
             copy(
-                out=packed_walk(x_bf[(g, h)], c0, c1, COPY_RUN),
-                in_=rows_walk(raw[:, :, first + c0 : first + c1], COPY_RUN),
+                out=packed_walk(x_bf[(g, h)], c0, c1, run),
+                in_=rows_walk(raw[:, :, first + c0 : first + c1], run),
             )
 
         def round_x_together(g, h, share=SCALAR_SHARE):
             round_x(nc.scalar.copy, g, h, 0, share)
-            round_x(nc.vector.tensor_copy, g, h, share, HALF)
+            round_x(nc.vector.tensor_copy, g, h, share, HALF, SUB_RUN)
 
         def multiply(which, g, m, h, c0=0, c1=HALF):
             i = OUT_TILES * g + m

@@ -30,6 +30,7 @@ HI_PAIR = -983056
 COPY_RUN = 4
 SUB_RUN = 2
 SCALAR_SHARE = 96
+WORD_TILES = (0,)
 GROUPS = ((0,), (1,), (2,), (3,), (4,), (5,), (6,), (7,), (8,), (9,), (10,), (11,))
 
 
@@ -59,7 +60,7 @@ def tile_mix_hilo_fm_silu_kernel(tc, w, x, b, out):
         banks = [(m, h) for h in (LEFT, RIGHT) for m in range(OUT_TILES)]
         acc = {(m, h): psum.tile([P, 2 * HALF], F32, name="acc" + str(2 * m + h)) for m, h in banks}
         res = {(m, h): sbuf("res" + str(2 * m + h), [P, HALF], F32) for m, h in banks}
-        hi_words = sbuf("hi_words", [P, PACK, P], F32)
+        hi_words = {i: sbuf("hi_words" + str(i), [P, PACK, P], F32) for i in WORD_TILES}
         b_rows = sbuf("b_rows", [P, P], F32)
         b_cols = sbuf("b_cols", [P, OUT_TILES], F32)
         ident = sbuf("ident", [P, P], F32)
@@ -112,27 +113,27 @@ def tile_mix_hilo_fm_silu_kernel(tc, w, x, b, out):
                 op0=ALU.bitwise_and,
             )
 
-        def mask_words(c0, c1):
-            raw, first = w_raw[0]
+        def mask_words(i, c0=0, c1=P):
+            raw, first = w_raw[i]
             nc.vector.tensor_scalar(
-                out=hi_words[:].bitcast(I32)[:, :, c0:c1],
+                out=hi_words[i][:].bitcast(I32)[:, :, c0:c1],
                 in0=raw[:].bitcast(I32)[:, :, first + c0 : first + c1],
                 scalar1=HI_WORD,
                 scalar2=None,
                 op0=ALU.bitwise_and,
             )
 
-        def subtract_words(c0, c1):
-            raw, first = w_raw[0]
+        def subtract_words(i, c0=0, c1=P):
+            raw, first = w_raw[i]
             nc.vector.tensor_tensor(
-                out=packed_walk(part(0, LO), c0, c1, SUB_RUN),
+                out=packed_walk(part(i, LO), c0, c1, SUB_RUN),
                 in0=rows_walk(raw[:, :, first + c0 : first + c1], SUB_RUN),
-                in1=rows_walk(hi_words[:, :, c0:c1], SUB_RUN),
+                in1=rows_walk(hi_words[i][:, :, c0:c1], SUB_RUN),
                 op=ALU.subtract,
             )
 
-        def copy_hi():
-            nc.scalar.copy(out=packed_walk(part(0, HI), 0, P, COPY_RUN), in_=rows_walk(hi_words[:], COPY_RUN))
+        def copy_hi(i):
+            nc.scalar.copy(out=packed_walk(part(i, HI), 0, P, COPY_RUN), in_=rows_walk(hi_words[i][:], COPY_RUN))
 
         def subtract(i, c0=0, c1=None):
             raw, first = w_raw[i]
@@ -215,68 +216,71 @@ def tile_mix_hilo_fm_silu_kernel(tc, w, x, b, out):
             nc.tensor.transpose(b_turn[:, 0:P], b_rows[:], ident[:])
 
             copy_top(1)
-            mask_words(0, 64)
-            mask_words(64, P)
-            subtract_words(0, 64)
-            subtract_words(64, P)
-            copy_hi()
-            for i in range(2, 8):
+            mask_words(0, 0, 64)
+            mask_words(0, 64, P)
+            subtract_words(0, 0, 64)
+            subtract_words(0, 64, P)
+            copy_top(2)
+            copy_top(3)
+            copy_hi(0)
+            for i in range(4, 8):
                 copy_top(i)
             round_x(nc.scalar.copy, 0, LEFT)
             round_x(nc.scalar.copy, 0, RIGHT)
             nc.scalar.copy(out=b_cols[:], in_=b_turn[:, 0:OUT_TILES])
-            for i in range(8, 12):
+            for i in range(8, 11):
                 copy_top(i)
             mask_top(1)
             quantize_part(0, LO)
             subtract(1)
-            quantize_part(0, HI)
-            quantize_part(1, HI)
             mask_top(2)
+            quantize_part(1, HI)
             quantize_part(1, LO)
-            subtract(2)
             mask_top(3)
-            quantize_part(2, HI)
-            quantize_part(2, LO)
+            subtract(2)
             subtract(3)
-            quantize_part(3, HI)
+            quantize_part(0, HI)
+            quantize_part(2, HI)
             mask_top(4)
-            quantize_part(3, LO)
+            quantize_part(2, LO)
+            quantize_w(3)
             subtract(4)
             mask_top(5)
             mask_top(6)
-            subtract(5)
             quantize_w(4)
+            subtract(5)
+            mask_top(7)
             subtract(6)
             quantize_x(0, LEFT)
             both_passes(0, LEFT, all_tiles)
-            mask_top(7)
             quantize_w(5)
             subtract(7)
+            quantize_w(6)
             quantize_x(0, RIGHT)
             both_passes(0, RIGHT, all_tiles)
             mask_top(8)
-            quantize_w(6)
+            quantize_w(7)
             subtract(8)
             mask_top(9)
-            quantize_w(7)
             round_x_together(1, LEFT, 96)
             round_x(nc.scalar.copy, 1, RIGHT)
-            mask_top(10)
-            quantize_w(8)
+            copy_top(11)
+            subtract(9)
             quantize_x(1, LEFT)
             both_passes(1, LEFT, all_tiles)
-            subtract(9)
-            mask_top(11)
+            quantize_w(8)
+            mask_top(10)
             quantize_x(1, RIGHT)
-            both_passes(1, RIGHT, all_tiles)
+            both_passes(1, RIGHT, range(last))
             round_x_together(2, LEFT, 96)
+            round_x(nc.scalar.copy, 2, RIGHT)
             quantize_w(9)
             quantize_x(2, LEFT)
             both_passes(2, LEFT, range(2))
-            round_x(nc.scalar.copy, 2, RIGHT)
+            both_passes(1, RIGHT, [last])
             subtract(10)
             quantize_part(10, HI)
+            mask_top(11)
             quantize_part(10, LO)
             both_passes(2, LEFT, [2])
             quantize_x(2, RIGHT)

@@ -218,74 +218,73 @@ def tile_mix_hilo_fm_silu_kernel(tc, w, x, b, out):
             copy_top(1)
             mask_words(0, 0, 64)
             mask_words(0, 64, P)
-            subtract_words(0, 0, 64)
-            subtract_words(0, 64, P)
-            copy_top(2)
-            copy_top(3)
             copy_hi(0)
-            for i in range(4, 8):
+            for i in range(2, 8):
                 copy_top(i)
             round_x(nc.scalar.copy, 0, LEFT)
             round_x(nc.scalar.copy, 0, RIGHT)
             nc.scalar.copy(out=b_cols[:], in_=b_turn[:, 0:OUT_TILES])
             for i in range(8, 11):
                 copy_top(i)
+            subtract_words(0, 0, 64)
             mask_top(1)
-            quantize_part(0, LO)
+            subtract_words(0, 64, P)
             subtract(1)
+            quantize_part(0, HI)
             mask_top(2)
+            quantize_part(0, LO)
             quantize_part(1, HI)
-            quantize_part(1, LO)
             mask_top(3)
+            quantize_part(1, LO)
             subtract(2)
             subtract(3)
-            quantize_part(0, HI)
             quantize_part(2, HI)
+            quantize_part(3, HI)
             mask_top(4)
             quantize_part(2, LO)
-            quantize_w(3)
-            subtract(4)
+            quantize_part(3, LO)
             mask_top(5)
+            subtract(4)
             mask_top(6)
-            quantize_w(4)
             subtract(5)
             mask_top(7)
+            quantize_w(4)
             subtract(6)
             quantize_x(0, LEFT)
             both_passes(0, LEFT, all_tiles)
             quantize_w(5)
             subtract(7)
-            quantize_w(6)
             quantize_x(0, RIGHT)
             both_passes(0, RIGHT, all_tiles)
+            quantize_w(6)
             mask_top(8)
             quantize_w(7)
-            subtract(8)
             mask_top(9)
-            round_x_together(1, LEFT, 96)
+            subtract(8)
+            round_x_together(1, LEFT)
             round_x(nc.scalar.copy, 1, RIGHT)
             copy_top(11)
+            mask_top(10)
             subtract(9)
             quantize_x(1, LEFT)
             both_passes(1, LEFT, all_tiles)
             quantize_w(8)
-            mask_top(10)
             quantize_x(1, RIGHT)
-            both_passes(1, RIGHT, range(last))
-            round_x_together(2, LEFT, 96)
+            both_passes(1, RIGHT, all_tiles)
+            round_x_together(2, LEFT)
             round_x(nc.scalar.copy, 2, RIGHT)
             quantize_w(9)
+            mask_top(11)
             quantize_x(2, LEFT)
             both_passes(2, LEFT, range(2))
-            both_passes(1, RIGHT, [last])
             subtract(10)
             quantize_part(10, HI)
-            mask_top(11)
-            quantize_part(10, LO)
-            both_passes(2, LEFT, [2])
             quantize_x(2, RIGHT)
-            both_passes(2, RIGHT, range(last))
+            both_passes(2, RIGHT, range(2))
             subtract(11)
+            quantize_part(10, LO)
+            for h in (LEFT, RIGHT):
+                both_passes(2, h, [2])
             quantize_part(11, HI)
             for h in (LEFT, RIGHT):
                 multiply(HI, 2, last, h)
@@ -293,7 +292,9 @@ def tile_mix_hilo_fm_silu_kernel(tc, w, x, b, out):
             for h in (LEFT, RIGHT):
                 multiply(LO, 2, last, h)
             for h in (LEFT, RIGHT):
-                for m in range(last):
+                for m in range(2):
                     finish(m, h, nc.sync)
+            for h in (LEFT, RIGHT):
+                finish(2, h, nc.sync)
             finish(last, LEFT, nc.sync)
             finish(last, RIGHT, nc.scalar)

@@ -29,7 +29,7 @@ HI_WORD = -1048576
 HI_PAIR = -983056
 COPY_RUN = 4
 SUB_RUN = 2
-SCALAR_SHARE = 96
+SCALAR_SHARE = 112
 WORD_TILES = (0,)
 GROUPS = ((0,), (1,), (2,), (3,), (4,), (5,), (6,), (7,), (8,), (9,), (10,), (11,))
 
@@ -218,8 +218,10 @@ def tile_mix_hilo_fm_silu_kernel(tc, w, x, b, out):
             copy_top(1)
             mask_words(0, 0, 64)
             mask_words(0, 64, P)
+            copy_top(2)
+            copy_top(3)
             copy_hi(0)
-            for i in range(2, 8):
+            for i in range(4, 8):
                 copy_top(i)
             round_x(nc.scalar.copy, 0, LEFT)
             round_x(nc.scalar.copy, 0, RIGHT)
@@ -230,18 +232,18 @@ def tile_mix_hilo_fm_silu_kernel(tc, w, x, b, out):
             mask_top(1)
             subtract_words(0, 64, P)
             subtract(1)
-            quantize_part(0, HI)
-            mask_top(2)
             quantize_part(0, LO)
+            mask_top(2)
             quantize_part(1, HI)
-            mask_top(3)
             quantize_part(1, LO)
             subtract(2)
-            subtract(3)
+            mask_top(3)
+            quantize_part(0, HI)
             quantize_part(2, HI)
-            quantize_part(3, HI)
-            mask_top(4)
             quantize_part(2, LO)
+            subtract(3)
+            mask_top(4)
+            quantize_part(3, HI)
             quantize_part(3, LO)
             mask_top(5)
             subtract(4)
@@ -265,26 +267,24 @@ def tile_mix_hilo_fm_silu_kernel(tc, w, x, b, out):
             round_x(nc.scalar.copy, 1, RIGHT)
             copy_top(11)
             mask_top(10)
-            subtract(9)
+            quantize_w(8)
             quantize_x(1, LEFT)
             both_passes(1, LEFT, all_tiles)
-            quantize_w(8)
+            subtract(9)
             quantize_x(1, RIGHT)
             both_passes(1, RIGHT, all_tiles)
             round_x_together(2, LEFT)
             round_x(nc.scalar.copy, 2, RIGHT)
-            quantize_w(9)
             mask_top(11)
-            quantize_x(2, LEFT)
-            both_passes(2, LEFT, range(2))
             subtract(10)
-            quantize_part(10, HI)
+            quantize_x(2, LEFT)
+            quantize_w(9)
+            both_passes(2, LEFT, range(2))
+            quantize_w(10)
+            both_passes(2, LEFT, [2])
             quantize_x(2, RIGHT)
-            both_passes(2, RIGHT, range(2))
+            both_passes(2, RIGHT, range(last))
             subtract(11)
-            quantize_part(10, LO)
-            for h in (LEFT, RIGHT):
-                both_passes(2, h, [2])
             quantize_part(11, HI)
             for h in (LEFT, RIGHT):
                 multiply(HI, 2, last, h)
@@ -292,9 +292,7 @@ def tile_mix_hilo_fm_silu_kernel(tc, w, x, b, out):
             for h in (LEFT, RIGHT):
                 multiply(LO, 2, last, h)
             for h in (LEFT, RIGHT):
-                for m in range(2):
+                for m in range(last):
                     finish(m, h, nc.sync)
-            for h in (LEFT, RIGHT):
-                finish(2, h, nc.sync)
             finish(last, LEFT, nc.sync)
             finish(last, RIGHT, nc.scalar)

@@ -25,13 +25,15 @@ HALF = T // 2
 LEFT, RIGHT = 0, 1
 HI, LO = 0, 1
 
+MX_ALIGN = 64
+DMA_ALIGN = 256
 HI_WORD = -1048576
 HI_PAIR = -983056
-COPY_RUN = 4
-SUB_RUN = 2
-SCALAR_SHARE = 112
-WORD_TILES = (0,)
-GROUPS = ((0,), (1,), (2,), (3,), (4,), (5,), (6,), (7,), (8,), (9,), (10,), (11,))
+SCALAR_RUN = 4
+VECTOR_RUN = 2
+SCALAR_SHARE = {1: 112, 2: 96}
+FIRST = 0
+CUT = P // 2
 
 
 def tile_mix_hilo_fm_silu_kernel(tc, w, x, b, out):
@@ -40,27 +42,26 @@ def tile_mix_hilo_fm_silu_kernel(tc, w, x, b, out):
         keep = ctx.enter_context(tc.tile_pool(name="keep", bufs=1))
         psum = ctx.enter_context(tc.psum_pool(name="psum", bufs=1))
 
-        def sbuf(name, shape, dtype):
-            return keep.tile(shape, dtype, name=name, align_bytes=64)
+        def sbuf(name, shape, dtype, align=MX_ALIGN):
+            return keep.tile(shape, dtype, name=name, align_bytes=align)
 
-        def per_group(name, width, dtype):
-            return {grp[0]: sbuf(name + str(grp[0]), [P, width * len(grp)], dtype) for grp in GROUPS}
+        def per_w_tile(name, width, dtype):
+            return [sbuf(name + str(i), [P, width], dtype) for i in range(W_TILES)]
 
-        def per_x_half(name, shape, dtype):
-            return {(g, h): sbuf(name + str(2 * g + h), shape, dtype) for g in range(PASSES) for h in (LEFT, RIGHT)}
+        def per_x_half(name, width, dtype):
+            return {(g, h): sbuf(name + str(2 * g + h), [P, width], dtype) for g in range(PASSES) for h in (LEFT, RIGHT)}
 
-        group_of = {i: grp for grp in GROUPS for i in grp}
-        w_top = per_group("w_top", P * PACK, BF16)
-        w_parts = per_group("w_parts", 2 * P * PACK, BF16)
-        w_codes = per_group("w_codes", 2 * P, U32)
-        w_scales = per_group("w_scales", 2 * P, U8)
-        x_bf = per_x_half("x_bf", [P, HALF * PACK], BF16)
-        x_codes = per_x_half("x_codes", [P, HALF], U32)
-        x_scales = per_x_half("x_scales", [P, HALF], U8)
+        w_top = per_w_tile("w_top", P * PACK, BF16)
+        w_parts = per_w_tile("w_parts", 2 * P * PACK, BF16)
+        w_codes = per_w_tile("w_codes", 2 * P, U32)
+        w_scales = per_w_tile("w_scales", 2 * P, U8)
+        x_bf = per_x_half("x_bf", HALF * PACK, BF16)
+        x_codes = per_x_half("x_codes", HALF, U32)
+        x_scales = per_x_half("x_scales", HALF, U8)
         banks = [(m, h) for h in (LEFT, RIGHT) for m in range(OUT_TILES)]
         acc = {(m, h): psum.tile([P, 2 * HALF], F32, name="acc" + str(2 * m + h)) for m, h in banks}
-        res = {(m, h): sbuf("res" + str(2 * m + h), [P, HALF], F32) for m, h in banks}
-        hi_words = {i: sbuf("hi_words" + str(i), [P, PACK, P], F32) for i in WORD_TILES}
+        res = {(m, h): sbuf("res" + str(2 * m + h), [P, HALF], F32, DMA_ALIGN) for m, h in banks}
+        hi_words = sbuf("hi_words0", [P, PACK, P], F32)
         b_rows = sbuf("b_rows", [P, P], F32)
         b_cols = sbuf("b_cols", [P, OUT_TILES], F32)
         ident = sbuf("ident", [P, P], F32)
@@ -70,7 +71,7 @@ def tile_mix_hilo_fm_silu_kernel(tc, w, x, b, out):
         x_raw = {}
 
         def load(src, name, g, c0, c1):
-            raw = sbuf(name, [P, PACK, c1 - c0], F32)
+            raw = sbuf(name, [P, PACK, c1 - c0], F32, DMA_ALIGN)
             rows = src[g * K_PASS : (g + 1) * K_PASS, c0:c1]
             nc.sync.dma_start(out=raw[:], in_=rows.rearrange("(p j) c -> p j c", j=PACK))
             return raw
@@ -91,103 +92,95 @@ def tile_mix_hilo_fm_silu_kernel(tc, w, x, b, out):
         def packed_walk(packed, c0, c1, run):
             return packed[:, PACK * c0 : PACK * c1].rearrange("p (c i j) -> p c j i", i=run, j=PACK)
 
-        def width(i):
-            return P * len(group_of[i])
-
         def part(i, which):
-            return w_parts[i][:, which * PACK * width(i) : (which + 1) * PACK * width(i)]
+            return w_parts[i][:, which * PACK * P : (which + 1) * PACK * P]
 
-        def copy_top(i, c0=0, c1=None):
+        def copy_top(i):
             raw, first = w_raw[i]
-            c1 = width(i) if c1 is None else c1
-            tops = raw[:].bitcast(BF16)[:, :, 2 * (first + c0) + 1 : 2 * (first + c1) : 2]
-            nc.scalar.activation(out=packed_walk(w_top[i], c0, c1, COPY_RUN), in_=rows_walk(tops, COPY_RUN), func=ACT.Copy)
+            tops = raw[:].bitcast(BF16)[:, :, 2 * first + 1 : 2 * (first + P) : 2]
+            nc.scalar.activation(
+                out=packed_walk(w_top[i], 0, P, SCALAR_RUN), in_=rows_walk(tops, SCALAR_RUN), func=ACT.Copy
+            )
 
-        def mask_top(i, c0=0, c1=None):
-            c1 = width(i) if c1 is None else c1
+        def mask_top(i):
             nc.vector.tensor_scalar(
-                out=part(i, HI)[:, PACK * c0 : PACK * c1].bitcast(I32),
-                in0=w_top[i][:, PACK * c0 : PACK * c1].bitcast(I32),
+                out=part(i, HI).bitcast(I32),
+                in0=w_top[i][:].bitcast(I32),
                 scalar1=HI_PAIR,
                 scalar2=None,
                 op0=ALU.bitwise_and,
             )
 
-        def mask_words(i, c0=0, c1=P):
+        def subtract(i, c0=0, c1=P):
             raw, first = w_raw[i]
+            nc.vector.tensor_tensor(
+                out=packed_walk(part(i, LO), c0, c1, VECTOR_RUN),
+                in0=rows_walk(raw[:, :, first + c0 : first + c1], VECTOR_RUN),
+                in1=packed_walk(part(i, HI), c0, c1, VECTOR_RUN),
+                op=ALU.subtract,
+            )
+
+        def mask_first(c0, c1):
+            raw, first = w_raw[FIRST]
             nc.vector.tensor_scalar(
-                out=hi_words[i][:].bitcast(I32)[:, :, c0:c1],
+                out=hi_words[:].bitcast(I32)[:, :, c0:c1],
                 in0=raw[:].bitcast(I32)[:, :, first + c0 : first + c1],
                 scalar1=HI_WORD,
                 scalar2=None,
                 op0=ALU.bitwise_and,
             )
 
-        def subtract_words(i, c0=0, c1=P):
-            raw, first = w_raw[i]
+        def subtract_first(c0, c1):
+            raw, first = w_raw[FIRST]
             nc.vector.tensor_tensor(
-                out=packed_walk(part(i, LO), c0, c1, SUB_RUN),
-                in0=rows_walk(raw[:, :, first + c0 : first + c1], SUB_RUN),
-                in1=rows_walk(hi_words[i][:, :, c0:c1], SUB_RUN),
+                out=packed_walk(part(FIRST, LO), c0, c1, VECTOR_RUN),
+                in0=rows_walk(raw[:, :, first + c0 : first + c1], VECTOR_RUN),
+                in1=rows_walk(hi_words[:, :, c0:c1], VECTOR_RUN),
                 op=ALU.subtract,
             )
 
-        def copy_hi(i):
-            nc.scalar.copy(out=packed_walk(part(i, HI), 0, P, COPY_RUN), in_=rows_walk(hi_words[i][:], COPY_RUN))
-
-        def subtract(i, c0=0, c1=None):
-            raw, first = w_raw[i]
-            c1 = width(i) if c1 is None else c1
-            nc.vector.tensor_tensor(
-                out=packed_walk(part(i, LO), c0, c1, SUB_RUN),
-                in0=rows_walk(raw[:, :, first + c0 : first + c1], SUB_RUN),
-                in1=packed_walk(part(i, HI), c0, c1, SUB_RUN),
-                op=ALU.subtract,
-            )
+        def pack_first_hi():
+            nc.scalar.copy(out=packed_walk(part(FIRST, HI), 0, P, SCALAR_RUN), in_=rows_walk(hi_words[:], SCALAR_RUN))
 
         def quantize_part(i, which):
-            cols = slice(which * width(i), (which + 1) * width(i))
+            cols = slice(which * P, (which + 1) * P)
             nc.vector.quantize_mx(out=w_codes[i][:, cols].bitcast(FP8X4), scales=w_scales[i][:, cols], in_=part(i, which))
 
         def quantize_w(i):
             nc.vector.quantize_mx(out=w_codes[i][:].bitcast(FP8X4), scales=w_scales[i][:], in_=w_parts[i][:])
 
-        def quantize_x(g, h, c0=0, c1=HALF):
-            nc.vector.quantize_mx(
-                out=x_codes[(g, h)][:, c0:c1].bitcast(FP8X4),
-                scales=x_scales[(g, h)][:, c0:c1],
-                in_=x_bf[(g, h)][:, PACK * c0 : PACK * c1],
-            )
+        def quantize_x(g, h):
+            nc.vector.quantize_mx(out=x_codes[(g, h)][:].bitcast(FP8X4), scales=x_scales[(g, h)][:], in_=x_bf[(g, h)][:])
 
-        def round_x(copy, g, h, c0=0, c1=HALF, run=COPY_RUN):
+        def round_x(copy, run, g, h, c0, c1):
             raw, first = x_raw[(g, h)]
-            copy(
-                out=packed_walk(x_bf[(g, h)], c0, c1, run),
-                in_=rows_walk(raw[:, :, first + c0 : first + c1], run),
-            )
+            copy(out=packed_walk(x_bf[(g, h)], c0, c1, run), in_=rows_walk(raw[:, :, first + c0 : first + c1], run))
 
-        def round_x_together(g, h, share=SCALAR_SHARE):
-            round_x(nc.scalar.copy, g, h, 0, share)
-            round_x(nc.vector.tensor_copy, g, h, share, HALF, SUB_RUN)
+        def round_x_scalar(g, h, c1=HALF):
+            round_x(nc.scalar.copy, SCALAR_RUN, g, h, 0, c1)
 
-        def multiply(which, g, m, h, c0=0, c1=HALF):
+        def round_x_shared(g):
+            round_x_scalar(g, LEFT, SCALAR_SHARE[g])
+            round_x(nc.vector.tensor_copy, VECTOR_RUN, g, LEFT, SCALAR_SHARE[g], HALF)
+            round_x_scalar(g, RIGHT)
+
+        def multiply(which, g, m, h):
             i = OUT_TILES * g + m
-            lead = group_of[i][0]
-            first = which * width(i) + (i - lead) * P
+            cols = slice(which * P, (which + 1) * P)
             nc.tensor.matmul_mx(
-                out=acc[(m, h)][:, c0:c1],
-                lhsT=w_codes[lead][:, first : first + P].bitcast(FP8X4),
-                lhsT_scale=w_scales[lead][:, first : first + P],
-                rhs=x_codes[(g, h)][:, c0:c1].bitcast(FP8X4),
-                rhs_scale=x_scales[(g, h)][:, c0:c1],
-                start=(g == 0 and which == HI and c0 == 0),
-                stop=(g == PASSES - 1 and which == LO and c1 == HALF),
+                out=acc[(m, h)][:, 0:HALF],
+                lhsT=w_codes[i][:, cols].bitcast(FP8X4),
+                lhsT_scale=w_scales[i][:, cols],
+                rhs=x_codes[(g, h)][:].bitcast(FP8X4),
+                rhs_scale=x_scales[(g, h)][:],
+                start=(g == 0 and which == HI),
+                stop=(g == PASSES - 1 and which == LO),
             )
 
-        def both_passes(g, h, out_tiles, c0=0, c1=HALF):
+        def both_products(g, h, out_tiles):
             for m in out_tiles:
-                multiply(HI, g, m, h, c0, c1)
-                multiply(LO, g, m, h, c0, c1)
+                multiply(HI, g, m, h)
+                multiply(LO, g, m, h)
 
         def finish(m, h, queue):
             nc.scalar.activation(
@@ -216,21 +209,22 @@ def tile_mix_hilo_fm_silu_kernel(tc, w, x, b, out):
             nc.tensor.transpose(b_turn[:, 0:P], b_rows[:], ident[:])
 
             copy_top(1)
-            mask_words(0, 0, 64)
-            mask_words(0, 64, P)
+            mask_first(0, CUT)
+            mask_first(CUT, P)
             copy_top(2)
             copy_top(3)
-            copy_hi(0)
-            for i in range(4, 8):
+            pack_first_hi()
+            for i in range(OUT_TILES, 2 * OUT_TILES):
                 copy_top(i)
-            round_x(nc.scalar.copy, 0, LEFT)
-            round_x(nc.scalar.copy, 0, RIGHT)
+            round_x_scalar(0, LEFT)
+            round_x_scalar(0, RIGHT)
             nc.scalar.copy(out=b_cols[:], in_=b_turn[:, 0:OUT_TILES])
-            for i in range(8, 11):
+            for i in range(2 * OUT_TILES, W_TILES - 1):
                 copy_top(i)
-            subtract_words(0, 0, 64)
+
+            subtract_first(0, CUT)
             mask_top(1)
-            subtract_words(0, 64, P)
+            subtract_first(CUT, P)
             subtract(1)
             quantize_part(0, LO)
             mask_top(2)
@@ -245,6 +239,7 @@ def tile_mix_hilo_fm_silu_kernel(tc, w, x, b, out):
             mask_top(4)
             quantize_part(3, HI)
             quantize_part(3, LO)
+
             mask_top(5)
             subtract(4)
             mask_top(6)
@@ -253,44 +248,44 @@ def tile_mix_hilo_fm_silu_kernel(tc, w, x, b, out):
             quantize_w(4)
             subtract(6)
             quantize_x(0, LEFT)
-            both_passes(0, LEFT, all_tiles)
+            both_products(0, LEFT, all_tiles)
             quantize_w(5)
             subtract(7)
             quantize_x(0, RIGHT)
-            both_passes(0, RIGHT, all_tiles)
+            both_products(0, RIGHT, all_tiles)
             quantize_w(6)
             mask_top(8)
             quantize_w(7)
             mask_top(9)
             subtract(8)
-            round_x_together(1, LEFT)
-            round_x(nc.scalar.copy, 1, RIGHT)
+
+            round_x_shared(1)
             copy_top(11)
             mask_top(10)
             quantize_w(8)
             quantize_x(1, LEFT)
-            both_passes(1, LEFT, all_tiles)
+            both_products(1, LEFT, all_tiles)
             subtract(9)
+            subtract(10, 0, CUT)
             quantize_x(1, RIGHT)
-            both_passes(1, RIGHT, all_tiles)
-            round_x_together(2, LEFT)
-            round_x(nc.scalar.copy, 2, RIGHT)
+            both_products(1, RIGHT, all_tiles)
+
+            round_x_shared(2)
             mask_top(11)
-            subtract(10)
+            subtract(10, CUT, P)
             quantize_x(2, LEFT)
             quantize_w(9)
-            both_passes(2, LEFT, range(2))
+            both_products(2, LEFT, range(last - 1))
             quantize_w(10)
-            both_passes(2, LEFT, [2])
+            both_products(2, LEFT, [last - 1])
             quantize_x(2, RIGHT)
-            both_passes(2, RIGHT, range(last))
+            both_products(2, RIGHT, range(last))
             subtract(11)
-            quantize_part(11, HI)
-            for h in (LEFT, RIGHT):
-                multiply(HI, 2, last, h)
-            quantize_part(11, LO)
-            for h in (LEFT, RIGHT):
-                multiply(LO, 2, last, h)
+            for which in (HI, LO):
+                quantize_part(11, which)
+                for h in (LEFT, RIGHT):
+                    multiply(which, 2, last, h)
+
             for h in (LEFT, RIGHT):
                 for m in range(last):
                     finish(m, h, nc.sync)

from contextlib import ExitStack

import concourse.mybir as mybir
from concourse.masks import make_identity

K, M, T = 1536, 512, 512
FLOPS = 2 * 2 * K * M * T

F32 = mybir.dt.float32
BF16 = mybir.dt.bfloat16
I32 = mybir.dt.int32
U32 = mybir.dt.uint32
U8 = mybir.dt.uint8
FP8X4 = mybir.dt.float8_e4m3fn_x4
ALU = mybir.AluOpType
ACT = mybir.ActivationFunctionType

P = 128
PACK = 4
K_PASS = P * PACK
PASSES = K // K_PASS
OUT_TILES = M // P
W_TILES = PASSES * OUT_TILES
HALF = T // 2
LEFT, RIGHT = 0, 1
HI, LO = 0, 1

MX_ALIGN = 64
DMA_ALIGN = 256
HI_WORD = -1048576
HI_PAIR = -983056
SCALAR_RUN = 4
VECTOR_RUN = 2
SCALAR_SHARE = {1: 112, 2: 96}
FIRST = 0
CUT = P // 2


def tile_mix_hilo_fm_silu_kernel(tc, w, x, b, out):
    nc = tc.nc
    with ExitStack() as ctx:
        keep = ctx.enter_context(tc.tile_pool(name="keep", bufs=1))
        psum = ctx.enter_context(tc.psum_pool(name="psum", bufs=1))

        def sbuf(name, shape, dtype, align=MX_ALIGN):
            return keep.tile(shape, dtype, name=name, align_bytes=align)

        def per_w_tile(name, width, dtype):
            return [sbuf(name + str(i), [P, width], dtype) for i in range(W_TILES)]

        def per_x_half(name, width, dtype):
            return {(g, h): sbuf(name + str(2 * g + h), [P, width], dtype) for g in range(PASSES) for h in (LEFT, RIGHT)}

        w_top = per_w_tile("w_top", P * PACK, BF16)
        w_parts = per_w_tile("w_parts", 2 * P * PACK, BF16)
        w_codes = per_w_tile("w_codes", 2 * P, U32)
        w_scales = per_w_tile("w_scales", 2 * P, U8)
        x_bf = per_x_half("x_bf", HALF * PACK, BF16)
        x_codes = per_x_half("x_codes", HALF, U32)
        x_scales = per_x_half("x_scales", HALF, U8)
        banks = [(m, h) for h in (LEFT, RIGHT) for m in range(OUT_TILES)]
        acc = {(m, h): psum.tile([P, 2 * HALF], F32, name="acc" + str(2 * m + h)) for m, h in banks}
        res = {(m, h): sbuf("res" + str(2 * m + h), [P, HALF], F32, DMA_ALIGN) for m, h in banks}
        hi_words = sbuf("hi_words0", [P, PACK, P], F32)
        b_rows = sbuf("b_rows", [P, P], F32)
        b_cols = sbuf("b_cols", [P, OUT_TILES], F32)
        ident = sbuf("ident", [P, P], F32)
        warm = sbuf("warm", [P, 2], F32)

        w_raw = {}
        x_raw = {}

        def load(src, name, g, c0, c1):
            raw = sbuf(name, [P, PACK, c1 - c0], F32, DMA_ALIGN)
            rows = src[g * K_PASS : (g + 1) * K_PASS, c0:c1]
            nc.sync.dma_start(out=raw[:], in_=rows.rearrange("(p j) c -> p j c", j=PACK))
            return raw

        def load_w(g, m0, m1):
            raw = load(w, "w_raw" + str(OUT_TILES * g + m0), g, m0 * P, m1 * P)
            for m in range(m0, m1):
                w_raw[OUT_TILES * g + m] = (raw, (m - m0) * P)

        def load_x(g):
            raw = load(x, "x_raw" + str(g), g, 0, T)
            for h in (LEFT, RIGHT):
                x_raw[(g, h)] = (raw, h * HALF)

        def rows_walk(rows, run):
            return rows.rearrange("p j (c i) -> p c j i", i=run)

        def packed_walk(packed, c0, c1, run):
            return packed[:, PACK * c0 : PACK * c1].rearrange("p (c i j) -> p c j i", i=run, j=PACK)

        def part(i, which):
            return w_parts[i][:, which * PACK * P : (which + 1) * PACK * P]

        def copy_top(i):
            raw, first = w_raw[i]
            tops = raw[:].bitcast(BF16)[:, :, 2 * first + 1 : 2 * (first + P) : 2]
            nc.scalar.activation(
                out=packed_walk(w_top[i], 0, P, SCALAR_RUN), in_=rows_walk(tops, SCALAR_RUN), func=ACT.Copy
            )

        def mask_top(i):
            nc.vector.tensor_scalar(
                out=part(i, HI).bitcast(I32),
                in0=w_top[i][:].bitcast(I32),
                scalar1=HI_PAIR,
                scalar2=None,
                op0=ALU.bitwise_and,
            )

        def subtract(i, c0=0, c1=P):
            raw, first = w_raw[i]
            nc.vector.tensor_tensor(
                out=packed_walk(part(i, LO), c0, c1, VECTOR_RUN),
                in0=rows_walk(raw[:, :, first + c0 : first + c1], VECTOR_RUN),
                in1=packed_walk(part(i, HI), c0, c1, VECTOR_RUN),
                op=ALU.subtract,
            )

        def mask_first(c0, c1):
            raw, first = w_raw[FIRST]
            nc.vector.tensor_scalar(
                out=hi_words[:].bitcast(I32)[:, :, c0:c1],
                in0=raw[:].bitcast(I32)[:, :, first + c0 : first + c1],
                scalar1=HI_WORD,
                scalar2=None,
                op0=ALU.bitwise_and,
            )

        def subtract_first(c0, c1):
            raw, first = w_raw[FIRST]
            nc.vector.tensor_tensor(
                out=packed_walk(part(FIRST, LO), c0, c1, VECTOR_RUN),
                in0=rows_walk(raw[:, :, first + c0 : first + c1], VECTOR_RUN),
                in1=rows_walk(hi_words[:, :, c0:c1], VECTOR_RUN),
                op=ALU.subtract,
            )

        def pack_first_hi():
            nc.scalar.copy(out=packed_walk(part(FIRST, HI), 0, P, SCALAR_RUN), in_=rows_walk(hi_words[:], SCALAR_RUN))

        def quantize_part(i, which):
            cols = slice(which * P, (which + 1) * P)
            nc.vector.quantize_mx(out=w_codes[i][:, cols].bitcast(FP8X4), scales=w_scales[i][:, cols], in_=part(i, which))

        def quantize_w(i):
            nc.vector.quantize_mx(out=w_codes[i][:].bitcast(FP8X4), scales=w_scales[i][:], in_=w_parts[i][:])

        def quantize_x(g, h):
            nc.vector.quantize_mx(out=x_codes[(g, h)][:].bitcast(FP8X4), scales=x_scales[(g, h)][:], in_=x_bf[(g, h)][:])

        def round_x(copy, run, g, h, c0, c1):
            raw, first = x_raw[(g, h)]
            copy(out=packed_walk(x_bf[(g, h)], c0, c1, run), in_=rows_walk(raw[:, :, first + c0 : first + c1], run))

        def round_x_scalar(g, h, c1=HALF):
            round_x(nc.scalar.copy, SCALAR_RUN, g, h, 0, c1)

        def round_x_shared(g):
            round_x_scalar(g, LEFT, SCALAR_SHARE[g])
            round_x(nc.vector.tensor_copy, VECTOR_RUN, g, LEFT, SCALAR_SHARE[g], HALF)
            round_x_scalar(g, RIGHT)

        def multiply(which, g, m, h):
            i = OUT_TILES * g + m
            cols = slice(which * P, (which + 1) * P)
            nc.tensor.matmul_mx(
                out=acc[(m, h)][:, 0:HALF],
                lhsT=w_codes[i][:, cols].bitcast(FP8X4),
                lhsT_scale=w_scales[i][:, cols],
                rhs=x_codes[(g, h)][:].bitcast(FP8X4),
                rhs_scale=x_scales[(g, h)][:],
                start=(g == 0 and which == HI),
                stop=(g == PASSES - 1 and which == LO),
            )

        def both_products(g, h, out_tiles):
            for m in out_tiles:
                multiply(HI, g, m, h)
                multiply(LO, g, m, h)

        def finish(m, h, queue):
            nc.scalar.activation(
                out=res[(m, h)][:], in_=acc[(m, h)][:, 0:HALF], func=ACT.Silu, bias=b_cols[:, m : m + 1], scale=1.0
            )
            queue.dma_start(out=out[m * P : (m + 1) * P, h * HALF : (h + 1) * HALF], in_=res[(m, h)][:])

        all_tiles = range(OUT_TILES)
        last = OUT_TILES - 1

        with tc.manual_schedule():
            load_w(0, 0, OUT_TILES // 2)
            load_w(0, OUT_TILES // 2, OUT_TILES)
            load_w(1, 0, OUT_TILES)
            load_x(0)
            load_w(2, 0, OUT_TILES)
            load_x(1)
            load_x(2)

            b_turn = acc[(last, RIGHT)]
            nc.vector.memset(b_rows[:], 0.0)
            nc.vector.memset(warm[:], 0.0)
            nc.scalar.dma_start(out=b_rows[0:OUT_TILES, :], in_=b.rearrange("(m p) -> m p", p=P))
            nc.scalar.activation(out=warm[:, 1:2], in_=warm[:, 0:1], func=ACT.Silu)
            make_identity(nc, ident[:])
            nc.tensor.transpose(b_turn[:, 0:P], b_rows[:], ident[:])

            copy_top(1)
            mask_first(0, CUT)
            mask_first(CUT, P)
            copy_top(2)
            copy_top(3)
            pack_first_hi()
            for i in range(OUT_TILES, 2 * OUT_TILES):
                copy_top(i)
            round_x_scalar(0, LEFT)
            round_x_scalar(0, RIGHT)
            nc.scalar.copy(out=b_cols[:], in_=b_turn[:, 0:OUT_TILES])
            for i in range(2 * OUT_TILES, W_TILES - 1):
                copy_top(i)

            subtract_first(0, CUT)
            mask_top(1)
            subtract_first(CUT, P)
            subtract(1)
            quantize_part(0, LO)
            mask_top(2)
            quantize_part(1, HI)
            quantize_part(1, LO)
            subtract(2)
            mask_top(3)
            quantize_part(0, HI)
            quantize_part(2, HI)
            quantize_part(2, LO)
            subtract(3)
            mask_top(4)
            quantize_part(3, HI)
            quantize_part(3, LO)

            mask_top(5)
            subtract(4)
            mask_top(6)
            subtract(5)
            mask_top(7)
            quantize_w(4)
            subtract(6)
            quantize_x(0, LEFT)
            both_products(0, LEFT, all_tiles)
            quantize_w(5)
            subtract(7)
            quantize_x(0, RIGHT)
            both_products(0, RIGHT, all_tiles)
            quantize_w(6)
            mask_top(8)
            quantize_w(7)
            mask_top(9)
            subtract(8)

            round_x_shared(1)
            copy_top(11)
            mask_top(10)
            quantize_w(8)
            quantize_x(1, LEFT)
            both_products(1, LEFT, all_tiles)
            subtract(9)
            subtract(10, 0, CUT)
            quantize_x(1, RIGHT)
            both_products(1, RIGHT, all_tiles)

            round_x_shared(2)
            mask_top(11)
            subtract(10, CUT, P)
            quantize_x(2, LEFT)
            quantize_w(9)
            both_products(2, LEFT, range(last - 1))
            quantize_w(10)
            both_products(2, LEFT, [last - 1])
            quantize_x(2, RIGHT)
            both_products(2, RIGHT, range(last))
            subtract(11)
            for which in (HI, LO):
                quantize_part(11, which)
                for h in (LEFT, RIGHT):
                    multiply(which, 2, last, h)

            for h in (LEFT, RIGHT):
                for m in range(last):
                    finish(m, h, nc.sync)
            finish(last, LEFT, nc.sync)
            finish(last, RIGHT, nc.scalar)
